import numpy as np
import ml_dtypes


def mxq(x, axis, fmt="e4m3"):
    dtype, down = {"e4m3": (ml_dtypes.float8_e4m3fn, 7), "e5m2": (ml_dtypes.float8_e5m2, 14)}[fmt]
    v = np.moveaxis(np.asarray(x, np.float32).astype(ml_dtypes.bfloat16).astype(np.float64), axis, -1)
    blocks = v.reshape(v.shape[:-1] + (-1, 32))
    amax = np.abs(blocks).max(-1, keepdims=True)
    byte = np.maximum(np.where(amax > 0, np.frexp(amax)[1] - 1 + 127, 0) - down, 1)
    scale = np.exp2(byte - 127.0)
    codes = (blocks / scale).astype(np.float32).astype(dtype).astype(np.float64)
    return np.moveaxis((codes * scale).reshape(v.shape), -1, axis)


WIDE = False


def mx_kscale(k):
    if not WIDE:
        return np.ones(k)
    levels = np.array([10, -10, 5, -5, 0])
    if k % 512:
        return np.exp2(np.random.permutation(np.resize(levels, k // 32))).repeat(32)
    a = np.empty((k // 512, 16))
    for p in range(k // 512):
        a[p, :8] = np.random.permutation(np.resize(levels, 8))
        for g in range(8):
            far = levels[np.abs(levels - a[p, g]) >= 10]
            a[p, g + 8] = far[np.random.randint(len(far))]
    return np.exp2(a.ravel()).repeat(32)


def f64(x):
    return np.asarray(x).astype(np.float64)


def striped(idx):
    return np.tile(idx.reshape(-1, 16).T, (8, 1)).astype(np.uint16)


def unstriped(offs):
    return offs[:16].T.reshape(-1).astype(np.int64)


def pack_weight(w):
    k, n = w.shape
    w = f64(np.asarray(w, np.float32).astype(ml_dtypes.bfloat16)).reshape(k // 32, 32, n)
    amax = np.abs(w).max(1)
    byte = np.clip(np.where(amax > 0, np.frexp(amax)[1] - 1 + 127 - 7, 1), 1, 254)
    scaled = (w * np.exp2(127.0 - byte)[:, None, :]).reshape(k, n).astype(np.float32)
    words = np.ascontiguousarray(scaled.reshape(k // 512, 128, 4, n).transpose(0, 1, 3, 2)).astype(ml_dtypes.float8_e4m3fn).view(np.uint8)
    return words, np.ascontiguousarray(byte.astype(np.uint8).reshape(k // 512, 16, n))


def unpack_weight(words, scales):
    g, p, n, _ = words.shape
    vals = np.ascontiguousarray(words).view(ml_dtypes.float8_e4m3fn).astype(np.float64) * np.repeat(np.exp2(scales.astype(np.float64) - 127.0), 8, axis=1)[..., None]
    return vals.transpose(0, 1, 3, 2).reshape(g * 512, n)


def gelu(v):
    return 0.5 * v * (1.0 + np.tanh(np.sqrt(2.0 / np.pi) * (v + 0.044715 * v**3)))

def planes(y):
    n, m = y.shape
    v = y.astype(np.float32).astype(ml_dtypes.bfloat16).astype(np.float64).reshape(n // 32, 32, m)
    top = np.abs(v).max(1)
    byte = np.clip(np.where(top > 0, np.frexp(top)[1] - 1 + 127 - 7, 1), 1, 254)
    codes = (v * np.exp2(127.0 - byte)[:, None, :]).reshape(n, m).astype(np.float32).astype(ml_dtypes.float8_e4m3fn).view(np.uint8)
    words = codes.reshape(n // 512, 128, 4, m).transpose(0, 1, 3, 2)
    return np.ascontiguousarray(words), np.ascontiguousarray(byte.astype(np.uint8).reshape(n // 512, 16, m))


K, T, D, H = 512, 512, 2, 512
P = 2 ** 7


def setup_inputs():
    n = np.random.standard_normal
    s = mx_kscale(K)[:, None]
    u = mx_kscale(H)
    packed_xT = pack_weight(n((K, T)) * s)
    return {
        "x_words": packed_xT[0],
        "x_scales": packed_xT[1],
        "w1": (n((K, H)) / np.sqrt(K) / s * u).astype(np.float32),
        "w2": (n((H, H)) / np.sqrt(H) / u[:, None]).astype(np.float32),
        "gate": (np.tile(np.random.uniform(0.2, 1.0, (D, 1, T)) / np.sqrt(D), (1, P, 1))).astype(np.float32),
        "pos1": striped(np.random.permutation(T)),
        "pos2": striped(np.random.permutation(T)),
    }


def reference(x_words, x_scales, w1, w2, gate, pos1, pos2):
    xq = unpack_weight(x_words, x_scales)
    h = gelu(mxq(f64(w1), 0, "e4m3").T @ xq)
    z = h - (h[:, unstriped(pos1)] * f64(gate)[0, :1] + h[:, unstriped(pos2)] * f64(gate)[1, :1])
    out_0 = mxq(f64(w2), 0, "e4m3").T @ mxq(z, 0, "e4m3")
    return (out_0,) + planes(out_0)

@@ -1,0 +1,290 @@
+from contextlib import ExitStack
+
+import concourse.mybir as mybir
+from concourse.masks import make_identity
+
+F32 = mybir.dt.float32
+BF16 = mybir.dt.bfloat16
+I32 = mybir.dt.int32
+U32 = mybir.dt.uint32
+U16 = mybir.dt.uint16
+U8 = mybir.dt.uint8
+FP8X4 = mybir.dt.float8_e4m3fn_x4
+MULT = mybir.AluOpType.mult
+GELU = mybir.ActivationFunctionType.Gelu_apprx_tanh
+
+P = 128
+PACK = 4
+N = 512
+BLOCKS = N // P
+FLOPS = 2 * 2 * 512 * 512 * 512
+CHUNKS = ((0, 1), (2,), (3,))
+
+
+def tile_picked_wlapl_gelu_lo_kernel(
+    tc, x_words, x_scales, w1, w2, gate, pos1, pos2, out_0, out_1, out_2
+):
+    nc = tc.nc
+    with ExitStack() as ctx:
+        keep = ctx.enter_context(tc.tile_pool(name="keep", bufs=1))
+        banks = ctx.enter_context(tc.psum_pool(name="banks", bufs=1))
+
+        def sb(shape, dtype, name, tag=None):
+            return keep.tile(shape, dtype, name=name, tag=tag or name, align_bytes=64)
+
+        def bank_tile(shape, name, number):
+            return banks.tile(shape, F32, name=name, tag="bank%d" % number)
+
+        gate_rows = sb([P, 8], F32, "gate_rows")
+        nc.sync.dma_start(
+            out=gate_rows[:],
+            in_=gate.rearrange("d r v -> (d r) v")[P - 1 : P + 1, :].rearrange("a (n j) -> (a n) j", j=8),
+        )
+        x_scale = sb([P, N], U8, "x_scale")
+        for q in range(4):
+            (nc.scalar if q else nc.sync).dma_start(
+                out=x_scale[:].bitcast(I32)[32 * q : 32 * q + 4, :],
+                in_=x_scales[0, 4 * q : 4 * q + 4, :].bitcast(I32),
+            )
+        w1_rows = w1.rearrange("(p j) i -> p j i", j=PACK)
+        w1_raw = [sb([P, PACK, P], F32, "w1_raw%d" % c) for c in range(BLOCKS)]
+        x_codes = sb([P, N], U32, "x_codes")
+        lists = [keep.tile([P, N // 16], U16, name="list%d" % d) for d in range(2)]
+        w2_raw = sb([P, PACK, N], F32, "w2_raw")
+        nc.sync.dma_start(out=w1_raw[0][:], in_=w1_rows[:, :, 0:P])
+        nc.sync.dma_start(
+            out=x_codes[:].bitcast(I32), in_=x_words[0].rearrange("p n t -> p (n t)").bitcast(I32)
+        )
+        for c in range(1, BLOCKS):
+            nc.sync.dma_start(out=w1_raw[c][:], in_=w1_rows[:, :, c * P : (c + 1) * P])
+        nc.sync.dma_start(lists[0][:], pos1)
+        nc.sync.dma_start(lists[1][:], pos2)
+        nc.sync.dma_start(out=w2_raw[:], in_=w2.rearrange("(p j) m -> p j m", j=PACK))
+
+        ident = sb([P, P], F32, "ident")
+        make_identity(nc, ident[:])
+
+        neg_rows = sb([P, 8], F32, "neg_rows")
+        nc.vector.tensor_scalar(neg_rows[:], gate_rows[:], -1.0, None, MULT)
+        neg_gate = sb([P, 2 * N], F32, "neg_gate")
+        for b in range(2):
+            bank = bank_tile([P, 4, P], "gate_bank%d" % b, b)
+            for j in range(4):
+                nc.tensor.transpose(
+                    bank[:, j, :], neg_rows[:, 4 * b + j : 4 * b + j + 1].to_broadcast([P, P]), ident[:]
+                )
+            nc.scalar.copy(
+                out=neg_gate[:].rearrange("p (n j) -> p n j", j=8)[:, :, 4 * b : 4 * b + 4],
+                in_=bank[:].rearrange("p j n -> p n j"),
+            )
+
+        h = [sb([P, N], F32, "h%d" % c) for c in range(BLOCKS)]
+        parts = {0: ((0, 4, 3),), 1: ((0, 4, 0),), 2: ((0, 2, 1), (2, 4, 3)), 3: ((0, 3, 2), (3, 4, 0))}
+        zt = {}
+        w1_bf = [sb([P, P, PACK], BF16, "w1_bf%d" % c) for c in range(BLOCKS)]
+
+        def cast_w1(c, on_vector):
+            src = w1_raw[c][:].rearrange("p j i -> p i j")
+            if on_vector:
+                nc.vector.tensor_copy(out=w1_bf[c][:], in_=src)
+            else:
+                nc.scalar.copy(out=w1_bf[c][:], in_=src)
+
+        def first_layer(c, numbers):
+            codes = sb([P, P], U32, "w1_codes%d" % c)
+            scale = sb([P, P], U8, "w1_scale%d" % c)
+            nc.vector.quantize_mx(
+                out=codes[:].bitcast(FP8X4), scales=scale[:], in_=w1_bf[c][:].rearrange("p i j -> p (i j)")
+            )
+            width = N // len(numbers)
+            for n, number in enumerate(numbers):
+                cols = slice(n * width, (n + 1) * width)
+                bank = bank_tile([P, width], "u%d_%d" % (c, n), number)
+                nc.tensor.matmul_mx(
+                    out=bank[:], lhsT=codes[:].bitcast(FP8X4), lhsT_scale=scale[:],
+                    rhs=x_codes[:, cols].bitcast(FP8X4), rhs_scale=x_scale[:, cols], start=True, stop=True,
+                )
+                nc.scalar.activation(h[c][:, cols], bank[:], GELU)
+
+        def add_turned(b, c, src, own, last):
+            c0, c1, number = [part for part in parts[b] if part[0] <= c < part[1]][0]
+            if own and c == c0:
+                zt[b, c0] = bank_tile([P, (c1 - c0) * P], "zt%d_%d" % (b, c0), number)
+            nc.tensor.matmul(
+                zt[b, c0][:, (c - c0) * P : (c - c0 + 1) * P], lhsT=src, rhs=ident[:], is_transpose=True,
+                start=own and c == c0, stop=last and c == c1 - 1,
+            )
+
+        def own_value(c, blocks):
+            for b in blocks:
+                add_turned(b, c, h[c][:, b * P : (b + 1) * P], True, False)
+
+        def neighbours(chunk, c, terms):
+            v0, width = chunk[0] * P, len(chunk) * P
+            for d in range(2):
+                nc.vector.tensor_tensor(
+                    terms[:, d, :],
+                    h[c][:].indirect(lists[d][:, v0 // 16 : (v0 + width) // 16]),
+                    neg_gate[:, d * N + v0 : d * N + v0 + width],
+                    MULT,
+                )
+                for n, b in enumerate(chunk):
+                    add_turned(b, c, terms[:, d, n * P : (n + 1) * P], False, d == 1)
+
+        w2_bf = sb([P, PACK, P, PACK], BF16, "w2_bf")
+        w2_codes = sb([P, N], U32, "w2_codes")
+        w2_scale = sb([P, N], U8, "w2_scale")
+
+        def cast_w2(t0):
+            nc.scalar.copy(
+                out=w2_bf[:, t0 : t0 + 2].rearrange("p t m j -> p m t j"),
+                in_=w2_raw[:].rearrange("p j (m t) -> p m t j", t=PACK)[:, :, t0 : t0 + 2],
+            )
+
+        def quantize_w2(t0):
+            cols = slice(t0 * P, (t0 + 2) * P)
+            nc.vector.quantize_mx(
+                out=w2_codes[:, cols].bitcast(FP8X4), scales=w2_scale[:, cols],
+                in_=w2_bf[:, t0 : t0 + 2].rearrange("p t m j -> p (t m j)"),
+            )
+
+        z_bf = {}
+        zt_bf = {}
+
+        def copy(engine, out, in_):
+            if engine is nc.vector:
+                engine.tensor_copy(out=out, in_=in_)
+            else:
+                engine.copy(out=out, in_=in_)
+
+        def round_part(b, k, engine, tag=None):
+            c0, c1, number = parts[b][k]
+            if k == 0:
+                zt_bf[b] = sb([P, 2, P, 2], BF16, "zt_bf%d" % b, tag)
+            copy(
+                engine,
+                out=zt_bf[b][:, :, 32 * c0 : 32 * c1, :],
+                in_=zt[b, c0][:].rearrange("v (p u e) -> v u p e", u=2, e=2),
+            )
+
+        def turn_back(b, number, engine):
+            words = zt_bf[b][:].rearrange("v u p e -> v (u p e)").bitcast(F32)
+            bank = bank_tile([P, 2, P], "back%d" % b, number)
+            for u in range(2):
+                nc.tensor.transpose(bank[:, u, :], words[:, u * P : (u + 1) * P], ident[:])
+            z_bf[b] = sb([P, P, PACK], BF16, "z_bf%d" % b)
+            copy(
+                engine,
+                out=z_bf[b][:].rearrange("p v t -> p (v t)").bitcast(F32).rearrange("p (v u) -> p v u", u=2),
+                in_=bank[:].rearrange("p u v -> p v u"),
+            )
+
+        y = [sb([P, PACK, P], F32, "y%d" % b) for b in range(BLOCKS)]
+        y_bf = sb([P, N, PACK], BF16, "y_bf")
+        acc = {}
+        y_rows = out_0.rearrange("(p t) v -> p t v", t=PACK)
+
+        z_mx = {}
+
+        def quantize_z(b):
+            codes = sb([P, P], U32, "z_codes%d" % b)
+            scale = sb([P, P], U8, "z_scale%d" % b)
+            nc.vector.quantize_mx(
+                out=codes[:].bitcast(FP8X4), scales=scale[:], in_=z_bf[b][:].rearrange("p v t -> p (v t)")
+            )
+            z_mx[b] = codes, scale
+
+        def second_layer(b, numbers):
+            codes, scale = z_mx[b]
+            per = PACK // len(numbers)
+            acc[b] = [bank_tile([P, per, P], "acc%d_%d" % (b, n), n) for n in numbers]
+            for t in range(PACK):
+                nc.tensor.matmul_mx(
+                    out=acc[b][t // per][:, t % per, :],
+                    lhsT=w2_codes[:, t * P : (t + 1) * P].bitcast(FP8X4),
+                    lhsT_scale=w2_scale[:, t * P : (t + 1) * P],
+                    rhs=codes[:].bitcast(FP8X4), rhs_scale=scale[:], start=True, stop=True,
+                )
+
+        def leave(b):
+            per = PACK // len(acc[b])
+            for n, bank in enumerate(acc[b]):
+                nc.scalar.copy(out=y[b][:, n * per : (n + 1) * per, :], in_=bank[:])
+            nc.sync.dma_start(out=y_rows[:, :, b * P : (b + 1) * P], in_=y[b][:])
+
+        def round_result(b, engine):
+            src = y[b] if engine is nc.vector else acc[b][0]
+            copy(engine, out=y_bf[:, b * P : (b + 1) * P, :], in_=src[:].rearrange("p t v -> p v t"))
+
+        y_scale = sb([P, N], U8, "y_scale")
+        y_words = out_1[0].rearrange("p n t -> p (n t)").bitcast(I32)
+
+        def quantize_result(b0, b1):
+            cols = slice(b0 * P, b1 * P)
+            nc.vector.quantize_mx(
+                out=y_codes[:, cols].bitcast(FP8X4), scales=y_scale[:, cols],
+                in_=y_bf[:, cols, :].rearrange("p v t -> p (v t)"),
+            )
+
+        V, S = nc.vector, nc.scalar
+        cast_w1(0, True)
+        first_layer(0, (2, 7))
+        cast_w1(1, True)
+        first_layer(1, (3,))
+        cast_w1(2, True)
+        first_layer(2, (0,))
+        cast_w1(3, False)
+        first_layer(3, (1,))
+        for c in range(BLOCKS):
+            own_value(c, (0, 1))
+            neighbours(CHUNKS[0], c, sb([P, 2, 2 * P], F32, "terms0_%d" % c))
+        cast_w2(0)
+        cast_w2(2)
+        terms1 = sb([P, BLOCKS, 2, P], F32, "terms1", "terms0_2")
+        round_part(0, 0, S)
+        round_part(1, 0, S)
+        turn_back(0, 2, S)
+        turn_back(1, 7, S)
+        for c in range(BLOCKS):
+            own_value(c, (2,))
+            neighbours(CHUNKS[1], c, terms1[:, c])
+        quantize_w2(0)
+        quantize_w2(2)
+        quantize_z(0)
+        second_layer(0, (4,))
+        quantize_z(1)
+        second_layer(1, (5,))
+        round_part(2, 0, S, "zt_bf1")
+        round_part(2, 1, S)
+        turn_back(2, 7, S)
+        leave(0)
+        round_result(0, S)
+        leave(1)
+        round_result(1, S)
+        terms2 = sb([P, BLOCKS, 2, P], F32, "terms2", "z_bf0")
+        for c in range(BLOCKS):
+            own_value(c, (3,))
+            neighbours(CHUNKS[2], c, terms2[:, c])
+        quantize_z(2)
+        second_layer(2, (6,))
+        round_part(3, 0, V)
+        round_part(3, 1, V)
+        turn_back(3, 1, V)
+        quantize_z(3)
+        second_layer(3, (4, 5))
+        leave(2)
+        round_result(2, S)
+        y_codes = sb([P, N], U32, "y_codes", "z_bf3")
+        quantize_result(0, 2)
+        quantize_result(2, 3)
+        leave(3)
+        round_result(3, V)
+        quantize_result(3, 4)
+        nc.sync.dma_start(out=y_words[:, 0 : 3 * P], in_=y_codes[:, 0 : 3 * P].bitcast(I32))
+        nc.sync.dma_start(out=y_words[:, 3 * P : N], in_=y_codes[:, 3 * P : N].bitcast(I32))
+        for q in range(4):
+            queue = nc.scalar if q % 2 else nc.sync
+            queue.dma_start(
+                out=out_2[0, 4 * q : 4 * q + 4, :].bitcast(I32),
+                in_=y_scale[:].bitcast(I32)[32 * q : 32 * q + 4, :],
+            )

@@ -1,7 +1,6 @@
 from contextlib import ExitStack
 
 import concourse.mybir as mybir
-from concourse.masks import make_identity
 
 F32 = mybir.dt.float32
 BF16 = mybir.dt.bfloat16
@@ -11,6 +10,9 @@ U16 = mybir.dt.uint16
 U8 = mybir.dt.uint8
 FP8X4 = mybir.dt.float8_e4m3fn_x4
 MULT = mybir.AluOpType.mult
+ADD = mybir.AluOpType.add
+IS_EQUAL = mybir.AluOpType.is_equal
+COPY = mybir.ActivationFunctionType.Copy
 GELU = mybir.ActivationFunctionType.Gelu_apprx_tanh
 
 P = 128
@@ -35,10 +37,16 @@ def tile_picked_wlapl_gelu_lo_kernel(
         def bank_tile(shape, name, number):
             return banks.tile(shape, F32, name=name, tag="bank%d" % number)
 
-        gate_rows = sb([P, 8], F32, "gate_rows")
+        def copy(engine, out, in_):
+            if engine is nc.vector:
+                engine.tensor_copy(out=out, in_=in_)
+            else:
+                engine.copy(out=out, in_=in_)
+
+        gate_rows = sb([P, 2, 4], F32, "gate_rows")
         nc.sync.dma_start(
             out=gate_rows[:],
-            in_=gate.rearrange("d r v -> (d r) v")[P - 1 : P + 1, :].rearrange("a (n j) -> (a n) j", j=8),
+            in_=gate[:, 0, :].rearrange("d (n j) -> n d j", j=4),
         )
         x_scale = sb([P, N], U8, "x_scale")
         for q in range(4):
@@ -47,61 +55,81 @@ def tile_picked_wlapl_gelu_lo_kernel(
                 in_=x_scales[0, 4 * q : 4 * q + 4, :].bitcast(I32),
             )
         w1_rows = w1.rearrange("(p j) i -> p j i", j=PACK)
-        w1_raw = [sb([P, PACK, P], F32, "w1_raw%d" % c) for c in range(BLOCKS)]
+        w1_raw = sb([P, PACK, N], F32, "w1_raw")
         x_codes = sb([P, N], U32, "x_codes")
         lists = [keep.tile([P, N // 16], U16, name="list%d" % d) for d in range(2)]
         w2_raw = sb([P, PACK, N], F32, "w2_raw")
-        nc.sync.dma_start(out=w1_raw[0][:], in_=w1_rows[:, :, 0:P])
+        nc.sync.dma_start(out=w1_raw[:], in_=w1_rows)
         nc.sync.dma_start(
             out=x_codes[:].bitcast(I32), in_=x_words[0].rearrange("p n t -> p (n t)").bitcast(I32)
         )
-        for c in range(1, BLOCKS):
-            nc.sync.dma_start(out=w1_raw[c][:], in_=w1_rows[:, :, c * P : (c + 1) * P])
         nc.sync.dma_start(lists[0][:], pos1)
         nc.sync.dma_start(lists[1][:], pos2)
         nc.sync.dma_start(out=w2_raw[:], in_=w2.rearrange("(p j) m -> p j m", j=PACK))
 
         ident = sb([P, P], F32, "ident")
-        make_identity(nc, ident[:])
+        ones = sb([P, P], F32, "ones")
+        column = sb([P, P], F32, "column")
+        in_quadrant = sb([P, 32], F32, "in_quadrant")
+        quadrant = sb([P, 1], F32, "quadrant")
+        row = sb([P, 1], F32, "row")
+        nc.vector.memset(ones[:], 1.0)
+        warm = sb([P, 1], F32, "warm")
+        nc.scalar.activation(warm[:], ones[:, 0:1], GELU)
+        nc.vector.tensor_tensor_scan(column[:], ones[:], ones[:], 0.0, MULT, ADD)
+        for q in range(4):
+            nc.vector.memset(quadrant[32 * q : 32 * q + 32, :], 32.0 * q)
+        nc.vector.transpose(in_quadrant[:], column[:, 0:32])
+        nc.vector.tensor_tensor(row[:], in_quadrant[:, 0:1], quadrant[:], ADD)
+        nc.vector.tensor_scalar(ident[:], column[:], row[:, 0:1], None, IS_EQUAL)
 
-        neg_rows = sb([P, 8], F32, "neg_rows")
-        nc.vector.tensor_scalar(neg_rows[:], gate_rows[:], -1.0, None, MULT)
-        neg_gate = sb([P, 2 * N], F32, "neg_gate")
-        for b in range(2):
-            bank = bank_tile([P, 4, P], "gate_bank%d" % b, b)
+        gate_banks = [bank_tile([P, 4, P], "gate_bank%d" % d, 4 + d) for d in range(2)]
+        for d in range(2):
             for j in range(4):
                 nc.tensor.transpose(
-                    bank[:, j, :], neg_rows[:, 4 * b + j : 4 * b + j + 1].to_broadcast([P, P]), ident[:]
+                    gate_banks[d][:, j, :], gate_rows[:, d, j : j + 1].to_broadcast([P, P]), ident[:]
                 )
-            nc.scalar.copy(
-                out=neg_gate[:].rearrange("p (n j) -> p n j", j=8)[:, :, 4 * b : 4 * b + 4],
-                in_=bank[:].rearrange("p j n -> p n j"),
+        neg_gate = [sb([P, N], F32, "neg_gate%d" % d) for d in range(2)]
+        for d in range(2):
+            nc.scalar.activation(
+                neg_gate[d][:].rearrange("p (n j) -> p n j", j=4),
+                gate_banks[d][:].rearrange("p j n -> p n j"),
+                COPY,
+                scale=-1.0,
             )
 
-        h = [sb([P, N], F32, "h%d" % c) for c in range(BLOCKS)]
-        parts = {0: ((0, 4, 3),), 1: ((0, 4, 0),), 2: ((0, 2, 1), (2, 4, 3)), 3: ((0, 3, 2), (3, 4, 0))}
+        h = {}
+        parts = {0: ((0, 4, 4),), 1: ((0, 4, 5),), 2: ((0, 2, 6), (2, 4, 4))}
         zt = {}
-        w1_bf = [sb([P, P, PACK], BF16, "w1_bf%d" % c) for c in range(BLOCKS)]
+        w1_mx = {}
+        w1_bf = {}
 
-        def cast_w1(c, on_vector):
-            src = w1_raw[c][:].rearrange("p j i -> p i j")
-            if on_vector:
-                nc.vector.tensor_copy(out=w1_bf[c][:], in_=src)
-            else:
-                nc.scalar.copy(out=w1_bf[c][:], in_=src)
-
-        def first_layer(c, numbers):
-            codes = sb([P, P], U32, "w1_codes%d" % c)
-            scale = sb([P, P], U8, "w1_scale%d" % c)
-            nc.vector.quantize_mx(
-                out=codes[:].bitcast(FP8X4), scales=scale[:], in_=w1_bf[c][:].rearrange("p i j -> p (i j)")
+        def cast_w1(t0, n, engine):
+            w1_bf[t0] = sb([P, n, P, PACK], BF16, "w1_bf%d" % t0)
+            copy(
+                engine,
+                out=w1_bf[t0][:].rearrange("p t m j -> p m t j"),
+                in_=w1_raw[:].rearrange("p j (m t) -> p m t j", t=PACK)[:, :, t0 : t0 + n],
             )
+
+        def quantize_w1(t0, n):
+            codes = sb([P, n * P], U32, "w1_codes%d" % t0)
+            scale = sb([P, n * P], U8, "w1_scale%d" % t0)
+            nc.vector.quantize_mx(
+                out=codes[:].bitcast(FP8X4), scales=scale[:], in_=w1_bf[t0][:].rearrange("p t m j -> p (t m j)")
+            )
+            for t in range(n):
+                w1_mx[t0 + t] = codes[:, t * P : (t + 1) * P], scale[:, t * P : (t + 1) * P]
+
+        def first_layer(c, numbers, tag=None):
+            codes, scale = w1_mx[c]
+            h[c] = sb([P, N], F32, "h%d" % c, tag)
             width = N // len(numbers)
             for n, number in enumerate(numbers):
                 cols = slice(n * width, (n + 1) * width)
                 bank = bank_tile([P, width], "u%d_%d" % (c, n), number)
                 nc.tensor.matmul_mx(
-                    out=bank[:], lhsT=codes[:].bitcast(FP8X4), lhsT_scale=scale[:],
+                    out=bank[:], lhsT=codes.bitcast(FP8X4), lhsT_scale=scale,
                     rhs=x_codes[:, cols].bitcast(FP8X4), rhs_scale=x_scale[:, cols], start=True, stop=True,
                 )
                 nc.scalar.activation(h[c][:, cols], bank[:], GELU)
@@ -125,11 +153,25 @@ def tile_picked_wlapl_gelu_lo_kernel(
                 nc.vector.tensor_tensor(
                     terms[:, d, :],
                     h[c][:].indirect(lists[d][:, v0 // 16 : (v0 + width) // 16]),
-                    neg_gate[:, d * N + v0 : d * N + v0 + width],
+                    neg_gate[d][:, v0 : v0 + width],
                     MULT,
                 )
                 for n, b in enumerate(chunk):
                     add_turned(b, c, terms[:, d, n * P : (n + 1) * P], False, d == 1)
+
+        def direct(b, terms, z, t, d):
+            cols = slice(b * P, (b + 1) * P)
+            nc.vector.tensor_tensor(
+                terms[:, d, t, :], h[t][:].indirect(lists[d][:, b * 8 : b * 8 + 8]), neg_gate[d][:, cols], MULT
+            )
+            if d == 0:
+                nc.vector.tensor_tensor(terms[:, 2, t, :], h[t][:, cols], terms[:, 0, t, :], ADD)
+            else:
+                nc.vector.tensor_tensor(z[:, t, :], terms[:, 2, t, :], terms[:, 1, t, :], ADD)
+
+        def round_z(b, z, engine):
+            z_bf[b] = sb([P, P, PACK], BF16, "z_bf%d" % b)
+            copy(engine, out=z_bf[b][:], in_=z[:].rearrange("p t v -> p v t"))
 
         w2_bf = sb([P, PACK, P, PACK], BF16, "w2_bf")
         w2_codes = sb([P, N], U32, "w2_codes")
@@ -151,20 +193,14 @@ def tile_picked_wlapl_gelu_lo_kernel(
         z_bf = {}
         zt_bf = {}
 
-        def copy(engine, out, in_):
-            if engine is nc.vector:
-                engine.tensor_copy(out=out, in_=in_)
-            else:
-                engine.copy(out=out, in_=in_)
-
         def round_part(b, k, engine, tag=None):
             c0, c1, number = parts[b][k]
             if k == 0:
                 zt_bf[b] = sb([P, 2, P, 2], BF16, "zt_bf%d" % b, tag)
             copy(
                 engine,
-                out=zt_bf[b][:, :, 32 * c0 : 32 * c1, :],
-                in_=zt[b, c0][:].rearrange("v (p u e) -> v u p e", u=2, e=2),
+                out=zt_bf[b][:, c0 // 2 : c1 // 2],
+                in_=zt[b, c0][:].rearrange("v (u e p) -> v u p e", e=2, p=P),
             )
 
         def turn_back(b, number, engine):
@@ -186,8 +222,8 @@ def tile_picked_wlapl_gelu_lo_kernel(
 
         z_mx = {}
 
-        def quantize_z(b):
-            codes = sb([P, P], U32, "z_codes%d" % b)
+        def quantize_z(b, tag=None):
+            codes = sb([P, P], U32, "z_codes%d" % b, tag)
             scale = sb([P, P], U8, "z_scale%d" % b)
             nc.vector.quantize_mx(
                 out=codes[:].bitcast(FP8X4), scales=scale[:], in_=z_bf[b][:].rearrange("p v t -> p (v t)")
@@ -227,20 +263,22 @@ def tile_picked_wlapl_gelu_lo_kernel(
             )
 
         V, S = nc.vector, nc.scalar
-        cast_w1(0, True)
+        cast_w1(0, 1, V)
+        cast_w1(2, 2, S)
+        quantize_w1(0, 1)
         first_layer(0, (2, 7))
-        cast_w1(1, True)
+        cast_w1(1, 1, V)
+        quantize_w1(1, 1)
         first_layer(1, (3,))
-        cast_w1(2, True)
+        quantize_w1(2, 2)
         first_layer(2, (0,))
-        cast_w1(3, False)
         first_layer(3, (1,))
         for c in range(BLOCKS):
             own_value(c, (0, 1))
             neighbours(CHUNKS[0], c, sb([P, 2, 2 * P], F32, "terms0_%d" % c))
         cast_w2(0)
         cast_w2(2)
-        terms1 = sb([P, BLOCKS, 2, P], F32, "terms1", "terms0_2")
+        terms1 = sb([P, BLOCKS, 2, P], F32, "terms1", "terms0_1")
         round_part(0, 0, S)
         round_part(1, 0, S)
         turn_back(0, 2, S)
@@ -251,31 +289,30 @@ def tile_picked_wlapl_gelu_lo_kernel(
         quantize_w2(0)
         quantize_w2(2)
         quantize_z(0)
-        second_layer(0, (4,))
+        second_layer(0, (3,))
         quantize_z(1)
-        second_layer(1, (5,))
+        second_layer(1, (0,))
         round_part(2, 0, S, "zt_bf1")
         round_part(2, 1, S)
-        turn_back(2, 7, S)
+        turn_back(2, 2, S)
         leave(0)
         round_result(0, S)
         leave(1)
         round_result(1, S)
-        terms2 = sb([P, BLOCKS, 2, P], F32, "terms2", "z_bf0")
-        for c in range(BLOCKS):
-            own_value(c, (3,))
-            neighbours(CHUNKS[2], c, terms2[:, c])
+        terms2 = sb([P, 3, BLOCKS, P], F32, "terms2", "z_bf0")
+        z3 = sb([P, BLOCKS, P], F32, "z3")
         quantize_z(2)
-        second_layer(2, (6,))
-        round_part(3, 0, V)
-        round_part(3, 1, V)
-        turn_back(3, 1, V)
-        quantize_z(3)
-        second_layer(3, (4, 5))
+        second_layer(2, (1,))
         leave(2)
-        round_result(2, S)
+        for d in range(2):
+            for c in range(BLOCKS):
+                direct(3, terms2, z3, c, d)
+        round_z(3, z3, V)
+        quantize_z(3)
+        second_layer(3, (3, 0))
         y_codes = sb([P, N], U32, "y_codes", "z_bf3")
         quantize_result(0, 2)
+        round_result(2, V)
         quantize_result(2, 3)
         leave(3)
         round_result(3, V)

@@ -16,11 +16,16 @@ COPY = mybir.ActivationFunctionType.Copy
 GELU = mybir.ActivationFunctionType.Gelu_apprx_tanh
 
 P = 128
-PACK = 4
+PLANES = 4
 N = 512
-BLOCKS = N // P
-FLOPS = 2 * 2 * 512 * 512 * 512
-CHUNKS = ((0, 1), (2,), (3,))
+QUADRANT = 32
+LISTS = 2
+PER_COLUMN = 16
+LAST = 3
+EARLY = 2
+FLOPS = 2 * 2 * N * N * N
+
+PARTS = {0: ((0, 4, 4),), 1: ((0, 4, 5),), 2: ((0, 2, 6), (2, 4, 5))}
 
 
 def tile_picked_wlapl_gelu_lo_kernel(
@@ -31,66 +36,61 @@ def tile_picked_wlapl_gelu_lo_kernel(
         keep = ctx.enter_context(tc.tile_pool(name="keep", bufs=1))
         banks = ctx.enter_context(tc.psum_pool(name="banks", bufs=1))
 
-        def sb(shape, dtype, name, tag=None):
-            return keep.tile(shape, dtype, name=name, tag=tag or name, align_bytes=64)
+        def sbuf(shape, dtype, name, after=None):
+            return keep.tile(shape, dtype, name=name, tag=after or name, align_bytes=64)
 
-        def bank_tile(shape, name, number):
-            return banks.tile(shape, F32, name=name, tag="bank%d" % number)
+        def psum(shape, name, bank):
+            return banks.tile(shape, F32, name=name, tag="bank%d" % bank)
 
         def copy(engine, out, in_):
             if engine is nc.vector:
-                engine.tensor_copy(out=out, in_=in_)
+                nc.vector.tensor_copy(out=out, in_=in_)
             else:
-                engine.copy(out=out, in_=in_)
+                nc.scalar.copy(out=out, in_=in_)
 
-        gate_rows = sb([P, 2, 4], F32, "gate_rows")
-        nc.sync.dma_start(
-            out=gate_rows[:],
-            in_=gate[:, 0, :].rearrange("d (n j) -> n d j", j=4),
-        )
-        x_scale = sb([P, N], U8, "x_scale")
+        def block(b):
+            return slice(b * P, (b + 1) * P)
+
+        gate_rows = sbuf([P, LISTS, 4], F32, "gate_rows")
+        nc.sync.dma_start(out=gate_rows[:], in_=gate[:, 0, :].rearrange("d (n j) -> n d j", j=4))
+        x_scale = sbuf([P, N], U8, "x_scale")
         for q in range(4):
-            (nc.scalar if q else nc.sync).dma_start(
-                out=x_scale[:].bitcast(I32)[32 * q : 32 * q + 4, :],
+            nc.scalar.dma_start(
+                out=x_scale[:].bitcast(I32)[QUADRANT * q : QUADRANT * q + 4, :],
                 in_=x_scales[0, 4 * q : 4 * q + 4, :].bitcast(I32),
             )
-        w1_rows = w1.rearrange("(p j) i -> p j i", j=PACK)
-        w1_raw = sb([P, PACK, N], F32, "w1_raw")
-        x_codes = sb([P, N], U32, "x_codes")
-        lists = [keep.tile([P, N // 16], U16, name="list%d" % d) for d in range(2)]
-        w2_raw = sb([P, PACK, N], F32, "w2_raw")
-        nc.sync.dma_start(out=w1_raw[:], in_=w1_rows)
-        nc.sync.dma_start(
-            out=x_codes[:].bitcast(I32), in_=x_words[0].rearrange("p n t -> p (n t)").bitcast(I32)
-        )
+        w1_raw = sbuf([P, PLANES, N], F32, "w1_raw")
+        x_codes = sbuf([P, N], U32, "x_codes")
+        lists = [keep.tile([P, N // PER_COLUMN], U16, name="list%d" % d) for d in range(LISTS)]
+        w2_raw = sbuf([P, PLANES, N], F32, "w2_raw")
+        nc.sync.dma_start(out=w1_raw[:], in_=w1.rearrange("(p j) i -> p j i", j=PLANES))
+        nc.sync.dma_start(out=x_codes[:].bitcast(I32), in_=x_words[0].rearrange("p n t -> p (n t)").bitcast(I32))
         nc.sync.dma_start(lists[0][:], pos1)
         nc.sync.dma_start(lists[1][:], pos2)
-        nc.sync.dma_start(out=w2_raw[:], in_=w2.rearrange("(p j) m -> p j m", j=PACK))
+        nc.sync.dma_start(out=w2_raw[:], in_=w2.rearrange("(p j) m -> p j m", j=PLANES))
 
-        ident = sb([P, P], F32, "ident")
-        ones = sb([P, P], F32, "ones")
-        column = sb([P, P], F32, "column")
-        in_quadrant = sb([P, 32], F32, "in_quadrant")
-        quadrant = sb([P, 1], F32, "quadrant")
-        row = sb([P, 1], F32, "row")
+        ident = sbuf([P, P], F32, "ident")
+        ones = sbuf([P, P], F32, "ones")
+        column = sbuf([P, P], F32, "column")
+        in_quadrant = sbuf([P, QUADRANT], F32, "in_quadrant")
+        quadrant_start = sbuf([P, 1], F32, "quadrant_start")
+        row = sbuf([P, 1], F32, "row")
         nc.vector.memset(ones[:], 1.0)
-        warm = sb([P, 1], F32, "warm")
+        warm = sbuf([P, 1], F32, "warm")
         nc.scalar.activation(warm[:], ones[:, 0:1], GELU)
         nc.vector.tensor_tensor_scan(column[:], ones[:], ones[:], 0.0, MULT, ADD)
         for q in range(4):
-            nc.vector.memset(quadrant[32 * q : 32 * q + 32, :], 32.0 * q)
-        nc.vector.transpose(in_quadrant[:], column[:, 0:32])
-        nc.vector.tensor_tensor(row[:], in_quadrant[:, 0:1], quadrant[:], ADD)
+            nc.vector.memset(quadrant_start[QUADRANT * q : QUADRANT * (q + 1), :], float(QUADRANT * q))
+        nc.vector.transpose(in_quadrant[:], column[:, 0:QUADRANT])
+        nc.vector.tensor_tensor(row[:], in_quadrant[:, 0:1], quadrant_start[:], ADD)
         nc.vector.tensor_scalar(ident[:], column[:], row[:, 0:1], None, IS_EQUAL)
 
-        gate_banks = [bank_tile([P, 4, P], "gate_bank%d" % d, 4 + d) for d in range(2)]
-        for d in range(2):
+        gate_banks = [psum([P, 4, P], "gate_bank%d" % d, 4 + d) for d in range(LISTS)]
+        for d in range(LISTS):
             for j in range(4):
-                nc.tensor.transpose(
-                    gate_banks[d][:, j, :], gate_rows[:, d, j : j + 1].to_broadcast([P, P]), ident[:]
-                )
-        neg_gate = [sb([P, N], F32, "neg_gate%d" % d) for d in range(2)]
-        for d in range(2):
+                nc.tensor.transpose(gate_banks[d][:, j, :], gate_rows[:, d, j : j + 1].to_broadcast([P, P]), ident[:])
+        neg_gate = [sbuf([P, N], F32, "neg_gate%d" % d) for d in range(LISTS)]
+        for d in range(LISTS):
             nc.scalar.activation(
                 neg_gate[d][:].rearrange("p (n j) -> p n j", j=4),
                 gate_banks[d][:].rearrange("p j n -> p n j"),
@@ -98,230 +98,190 @@ def tile_picked_wlapl_gelu_lo_kernel(
                 scale=-1.0,
             )
 
-        h = {}
-        parts = {0: ((0, 4, 4),), 1: ((0, 4, 5),), 2: ((0, 2, 6), (2, 4, 4))}
-        zt = {}
-        w1_mx = {}
-        w1_bf = {}
-
-        def cast_w1(t0, n, engine):
-            w1_bf[t0] = sb([P, n, P, PACK], BF16, "w1_bf%d" % t0)
+        def round_weights(engine, rounded, raw, t0, count):
             copy(
                 engine,
-                out=w1_bf[t0][:].rearrange("p t m j -> p m t j"),
-                in_=w1_raw[:].rearrange("p j (m t) -> p m t j", t=PACK)[:, :, t0 : t0 + n],
+                out=rounded.rearrange("p t c j -> p c t j"),
+                in_=raw[:].rearrange("p j (c t) -> p c t j", t=PLANES)[:, :, t0 : t0 + count],
             )
 
-        def quantize_w1(t0, n):
-            codes = sb([P, n * P], U32, "w1_codes%d" % t0)
-            scale = sb([P, n * P], U8, "w1_scale%d" % t0)
-            nc.vector.quantize_mx(
-                out=codes[:].bitcast(FP8X4), scales=scale[:], in_=w1_bf[t0][:].rearrange("p t m j -> p (t m j)")
+        def quantize(codes, scale, rounded):
+            nc.vector.quantize_mx(out=codes.bitcast(FP8X4), scales=scale, in_=rounded)
+
+        def product(out, w_codes, w_scale, codes, scale):
+            nc.tensor.matmul_mx(
+                out=out, lhsT=w_codes.bitcast(FP8X4), lhsT_scale=w_scale,
+                rhs=codes.bitcast(FP8X4), rhs_scale=scale, start=True, stop=True,
             )
-            for t in range(n):
-                w1_mx[t0 + t] = codes[:, t * P : (t + 1) * P], scale[:, t * P : (t + 1) * P]
 
-        def first_layer(c, numbers, tag=None):
-            codes, scale = w1_mx[c]
-            h[c] = sb([P, N], F32, "h%d" % c, tag)
-            width = N // len(numbers)
-            for n, number in enumerate(numbers):
-                cols = slice(n * width, (n + 1) * width)
-                bank = bank_tile([P, width], "u%d_%d" % (c, n), number)
-                nc.tensor.matmul_mx(
-                    out=bank[:], lhsT=codes.bitcast(FP8X4), lhsT_scale=scale,
-                    rhs=x_codes[:, cols].bitcast(FP8X4), rhs_scale=x_scale[:, cols], start=True, stop=True,
-                )
-                nc.scalar.activation(h[c][:, cols], bank[:], GELU)
+        w1_bf, w1_mx, h = {}, {}, {}
 
-        def add_turned(b, c, src, own, last):
-            c0, c1, number = [part for part in parts[b] if part[0] <= c < part[1]][0]
-            if own and c == c0:
-                zt[b, c0] = bank_tile([P, (c1 - c0) * P], "zt%d_%d" % (b, c0), number)
+        def round_w1(t0, count, engine):
+            w1_bf[t0] = sbuf([P, count, P, PLANES], BF16, "w1_bf%d" % t0)
+            round_weights(engine, w1_bf[t0][:], w1_raw, t0, count)
+
+        def quantize_w1(t0, count):
+            codes = sbuf([P, count * P], U32, "w1_codes%d" % t0)
+            scale = sbuf([P, count * P], U8, "w1_scale%d" % t0)
+            quantize(codes[:], scale[:], w1_bf[t0][:].rearrange("p t c j -> p (t c j)"))
+            for t in range(count):
+                w1_mx[t0 + t] = codes[:, block(t)], scale[:, block(t)]
+
+        def first_layer(t, bank_numbers):
+            h[t] = sbuf([P, N], F32, "h%d" % t)
+            width = N // len(bank_numbers)
+            for n, bank in enumerate(bank_numbers):
+                nodes = slice(n * width, (n + 1) * width)
+                pre = psum([P, width], "pre%d_%d" % (t, n), bank)
+                product(pre[:], w1_mx[t][0], w1_mx[t][1], x_codes[:, nodes], x_scale[:, nodes])
+                nc.scalar.activation(h[t][:, nodes], pre[:], GELU)
+
+        zt, zt_bf, z_bf = {}, {}, {}
+
+        def gather(term, t, d, v0, v1):
+            window = h[t][:].indirect(lists[d][:, v0 // PER_COLUMN : v1 // PER_COLUMN])
+            nc.vector.tensor_tensor(term, window, neg_gate[d][:, v0:v1], MULT)
+
+        def add_turned(b, t, src, own, last):
+            t0, t1, bank = [part for part in PARTS[b] if part[0] <= t < part[1]][0]
+            if own and t == t0:
+                zt[b, t0] = psum([P, (t1 - t0) * P], "zt%d_%d" % (b, t0), bank)
             nc.tensor.matmul(
-                zt[b, c0][:, (c - c0) * P : (c - c0 + 1) * P], lhsT=src, rhs=ident[:], is_transpose=True,
-                start=own and c == c0, stop=last and c == c1 - 1,
+                zt[b, t0][:, block(t - t0)], lhsT=src, rhs=ident[:], is_transpose=True,
+                start=own and t == t0, stop=last and t == t1 - 1,
             )
 
-        def own_value(c, blocks):
+        def sum_by_transposes(blocks, t, terms):
             for b in blocks:
-                add_turned(b, c, h[c][:, b * P : (b + 1) * P], True, False)
+                add_turned(b, t, h[t][:, block(b)], True, False)
+            for d in range(LISTS):
+                gather(terms[:, d, :], t, d, blocks[0] * P, (blocks[-1] + 1) * P)
+                for n, b in enumerate(blocks):
+                    add_turned(b, t, terms[:, d, block(n)], False, d == LISTS - 1)
 
-        def neighbours(chunk, c, terms):
-            v0, width = chunk[0] * P, len(chunk) * P
-            for d in range(2):
-                nc.vector.tensor_tensor(
-                    terms[:, d, :],
-                    h[c][:].indirect(lists[d][:, v0 // 16 : (v0 + width) // 16]),
-                    neg_gate[d][:, v0 : v0 + width],
-                    MULT,
+        def round_turned(b, after=None):
+            zt_bf[b] = sbuf([P, 2, P, 2], BF16, "zt_bf%d" % b, after)
+            for t0, t1, bank in PARTS[b]:
+                nc.scalar.copy(
+                    out=zt_bf[b][:, t0 // 2 : t1 // 2],
+                    in_=zt[b, t0][:].rearrange("v (u e p) -> v u p e", e=2, p=P),
                 )
-                for n, b in enumerate(chunk):
-                    add_turned(b, c, terms[:, d, n * P : (n + 1) * P], False, d == 1)
 
-        def direct(b, terms, z, t, d):
-            cols = slice(b * P, (b + 1) * P)
-            nc.vector.tensor_tensor(
-                terms[:, d, t, :], h[t][:].indirect(lists[d][:, b * 8 : b * 8 + 8]), neg_gate[d][:, cols], MULT
-            )
-            if d == 0:
-                nc.vector.tensor_tensor(terms[:, 2, t, :], h[t][:, cols], terms[:, 0, t, :], ADD)
-            else:
-                nc.vector.tensor_tensor(z[:, t, :], terms[:, 2, t, :], terms[:, 1, t, :], ADD)
-
-        def round_z(b, z, engine):
-            z_bf[b] = sb([P, P, PACK], BF16, "z_bf%d" % b)
-            copy(engine, out=z_bf[b][:], in_=z[:].rearrange("p t v -> p v t"))
-
-        w2_bf = sb([P, PACK, P, PACK], BF16, "w2_bf")
-        w2_codes = sb([P, N], U32, "w2_codes")
-        w2_scale = sb([P, N], U8, "w2_scale")
-
-        def cast_w2(t0):
-            nc.scalar.copy(
-                out=w2_bf[:, t0 : t0 + 2].rearrange("p t m j -> p m t j"),
-                in_=w2_raw[:].rearrange("p j (m t) -> p m t j", t=PACK)[:, :, t0 : t0 + 2],
-            )
-
-        def quantize_w2(t0):
-            cols = slice(t0 * P, (t0 + 2) * P)
-            nc.vector.quantize_mx(
-                out=w2_codes[:, cols].bitcast(FP8X4), scales=w2_scale[:, cols],
-                in_=w2_bf[:, t0 : t0 + 2].rearrange("p t m j -> p (t m j)"),
-            )
-
-        z_bf = {}
-        zt_bf = {}
-
-        def round_part(b, k, engine, tag=None):
-            c0, c1, number = parts[b][k]
-            if k == 0:
-                zt_bf[b] = sb([P, 2, P, 2], BF16, "zt_bf%d" % b, tag)
-            copy(
-                engine,
-                out=zt_bf[b][:, c0 // 2 : c1 // 2],
-                in_=zt[b, c0][:].rearrange("v (u e p) -> v u p e", e=2, p=P),
-            )
-
-        def turn_back(b, number, engine):
-            words = zt_bf[b][:].rearrange("v u p e -> v (u p e)").bitcast(F32)
-            bank = bank_tile([P, 2, P], "back%d" % b, number)
+        def turn_back(b, bank):
+            pairs = zt_bf[b][:].rearrange("v u p e -> v (u p e)").bitcast(F32)
+            back = psum([P, 2, P], "back%d" % b, bank)
             for u in range(2):
-                nc.tensor.transpose(bank[:, u, :], words[:, u * P : (u + 1) * P], ident[:])
-            z_bf[b] = sb([P, P, PACK], BF16, "z_bf%d" % b)
-            copy(
-                engine,
+                nc.tensor.transpose(back[:, u, :], pairs[:, block(u)], ident[:])
+            z_bf[b] = sbuf([P, P, PLANES], BF16, "z_bf%d" % b)
+            nc.scalar.copy(
                 out=z_bf[b][:].rearrange("p v t -> p (v t)").bitcast(F32).rearrange("p (v u) -> p v u", u=2),
-                in_=bank[:].rearrange("p u v -> p v u"),
+                in_=back[:].rearrange("p u v -> p v u"),
             )
 
-        y = [sb([P, PACK, P], F32, "y%d" % b) for b in range(BLOCKS)]
-        y_bf = sb([P, N, PACK], BF16, "y_bf")
-        acc = {}
-        y_rows = out_0.rearrange("(p t) v -> p t v", t=PACK)
+        w2_bf = sbuf([P, PLANES, P, PLANES], BF16, "w2_bf")
+        w2_codes = sbuf([P, N], U32, "w2_codes")
+        w2_scale = sbuf([P, N], U8, "w2_scale")
+        y = [sbuf([P, PLANES, P], F32, "y%d" % b) for b in range(N // P)]
+        y_bf = sbuf([P, N, PLANES], BF16, "y_bf")
+        y_scale = sbuf([P, N], U8, "y_scale")
+        y_rows = out_0.rearrange("(p t) v -> p t v", t=PLANES)
+        y_words = out_1[0].rearrange("p n t -> p (n t)").bitcast(I32)
+        z_mx, acc = {}, {}
 
-        z_mx = {}
-
-        def quantize_z(b, tag=None):
-            codes = sb([P, P], U32, "z_codes%d" % b, tag)
-            scale = sb([P, P], U8, "z_scale%d" % b)
-            nc.vector.quantize_mx(
-                out=codes[:].bitcast(FP8X4), scales=scale[:], in_=z_bf[b][:].rearrange("p v t -> p (v t)")
-            )
+        def quantize_z(b):
+            codes = sbuf([P, P], U32, "z_codes%d" % b)
+            scale = sbuf([P, P], U8, "z_scale%d" % b)
+            quantize(codes[:], scale[:], z_bf[b][:].rearrange("p v t -> p (v t)"))
             z_mx[b] = codes, scale
 
-        def second_layer(b, numbers):
-            codes, scale = z_mx[b]
-            per = PACK // len(numbers)
-            acc[b] = [bank_tile([P, per, P], "acc%d_%d" % (b, n), n) for n in numbers]
-            for t in range(PACK):
-                nc.tensor.matmul_mx(
-                    out=acc[b][t // per][:, t % per, :],
-                    lhsT=w2_codes[:, t * P : (t + 1) * P].bitcast(FP8X4),
-                    lhsT_scale=w2_scale[:, t * P : (t + 1) * P],
-                    rhs=codes[:].bitcast(FP8X4), rhs_scale=scale[:], start=True, stop=True,
+        def second_layer(b, bank_numbers):
+            per_bank = PLANES // len(bank_numbers)
+            acc[b] = [psum([P, per_bank, P], "acc%d_%d" % (b, bank), bank) for bank in bank_numbers]
+            for t in range(PLANES):
+                product(
+                    acc[b][t // per_bank][:, t % per_bank, :],
+                    w2_codes[:, block(t)], w2_scale[:, block(t)], z_mx[b][0][:], z_mx[b][1][:],
                 )
 
-        def leave(b):
-            per = PACK // len(acc[b])
-            for n, bank in enumerate(acc[b]):
-                nc.scalar.copy(out=y[b][:, n * per : (n + 1) * per, :], in_=bank[:])
-            nc.sync.dma_start(out=y_rows[:, :, b * P : (b + 1) * P], in_=y[b][:])
+        def store_result(b):
+            per_bank = PLANES // len(acc[b])
+            for n, sums in enumerate(acc[b]):
+                nc.scalar.copy(out=y[b][:, n * per_bank : (n + 1) * per_bank, :], in_=sums[:])
+            nc.sync.dma_start(out=y_rows[:, :, block(b)], in_=y[b][:])
 
-        def round_result(b, engine):
-            src = y[b] if engine is nc.vector else acc[b][0]
-            copy(engine, out=y_bf[:, b * P : (b + 1) * P, :], in_=src[:].rearrange("p t v -> p v t"))
+        def round_result(b, engine, src):
+            copy(engine, out=y_bf[:, block(b), :], in_=src[:].rearrange("p t v -> p v t"))
 
-        y_scale = sb([P, N], U8, "y_scale")
-        y_words = out_1[0].rearrange("p n t -> p (n t)").bitcast(I32)
-
-        def quantize_result(b0, b1):
-            cols = slice(b0 * P, b1 * P)
-            nc.vector.quantize_mx(
-                out=y_codes[:, cols].bitcast(FP8X4), scales=y_scale[:, cols],
-                in_=y_bf[:, cols, :].rearrange("p v t -> p (v t)"),
-            )
-
-        V, S = nc.vector, nc.scalar
-        cast_w1(0, 1, V)
-        cast_w1(2, 2, S)
+        round_w1(0, 1, nc.vector)
+        round_w1(2, 2, nc.scalar)
         quantize_w1(0, 1)
         first_layer(0, (2, 7))
-        cast_w1(1, 1, V)
+        round_w1(1, 1, nc.vector)
         quantize_w1(1, 1)
         first_layer(1, (3,))
         quantize_w1(2, 2)
         first_layer(2, (0,))
         first_layer(3, (1,))
-        for c in range(BLOCKS):
-            own_value(c, (0, 1))
-            neighbours(CHUNKS[0], c, sb([P, 2, 2 * P], F32, "terms0_%d" % c))
-        cast_w2(0)
-        cast_w2(2)
-        terms1 = sb([P, BLOCKS, 2, P], F32, "terms1", "terms0_1")
-        round_part(0, 0, S)
-        round_part(1, 0, S)
-        turn_back(0, 2, S)
-        turn_back(1, 7, S)
-        for c in range(BLOCKS):
-            own_value(c, (2,))
-            neighbours(CHUNKS[1], c, terms1[:, c])
-        quantize_w2(0)
-        quantize_w2(2)
+
+        for t in range(PLANES):
+            sum_by_transposes((0, 1), t, sbuf([P, LISTS, 2 * P], F32, "terms01_%d" % t))
+        for t0 in (0, 2):
+            round_weights(nc.scalar, w2_bf[:, t0 : t0 + 2], w2_raw, t0, 2)
+        terms2 = sbuf([P, PLANES, LISTS, P], F32, "terms2", after="terms01_1")
+        round_turned(0)
+        round_turned(1)
+        turn_back(0, 2)
+        turn_back(1, 7)
+        for t in range(PLANES):
+            sum_by_transposes((2,), t, terms2[:, t])
+        quantize(w2_codes[:], w2_scale[:], w2_bf[:].rearrange("p t c j -> p (t c j)"))
         quantize_z(0)
         second_layer(0, (3,))
         quantize_z(1)
-        second_layer(1, (0,))
-        round_part(2, 0, S, "zt_bf1")
-        round_part(2, 1, S)
-        turn_back(2, 2, S)
-        leave(0)
-        round_result(0, S)
-        leave(1)
-        round_result(1, S)
-        terms2 = sb([P, 3, BLOCKS, P], F32, "terms2", "z_bf0")
-        z3 = sb([P, BLOCKS, P], F32, "z3")
+        round_turned(2, after="zt_bf1")
+        turn_back(2, 2)
+        second_layer(1, (5,))
+        for b in range(2):
+            store_result(b)
+            round_result(b, nc.scalar, acc[b][0])
+
+        early = sbuf([P, EARLY, P], F32, "early", after="zt_bf0")
+        late = sbuf([P, LISTS * PLANES - EARLY, P], F32, "late", after="z_bf0")
+        with_first = sbuf([P, PLANES, P], F32, "with_first")
+        z_last = sbuf([P, PLANES, P], F32, "z_last")
+        second = late[:, PLANES - EARLY :, :]
+        for t in range(PLANES):
+            term = early[:, t, :] if t < EARLY else late[:, t - EARLY, :]
+            gather(term, t, 0, LAST * P, N)
+            nc.vector.tensor_tensor(with_first[:, t, :], h[t][:, block(LAST)], term, ADD)
+        for t in range(PLANES):
+            gather(second[:, t, :], t, 1, LAST * P, N)
+        for planes in (slice(0, PLANES - 1), slice(PLANES - 1, PLANES)):
+            nc.vector.tensor_tensor(z_last[:, planes, :], with_first[:, planes, :], second[:, planes, :], ADD)
         quantize_z(2)
         second_layer(2, (1,))
-        leave(2)
-        for d in range(2):
-            for c in range(BLOCKS):
-                direct(3, terms2, z3, c, d)
-        round_z(3, z3, V)
-        quantize_z(3)
-        second_layer(3, (3, 0))
-        y_codes = sb([P, N], U32, "y_codes", "z_bf3")
-        quantize_result(0, 2)
-        round_result(2, V)
-        quantize_result(2, 3)
-        leave(3)
-        round_result(3, V)
-        quantize_result(3, 4)
-        nc.sync.dma_start(out=y_words[:, 0 : 3 * P], in_=y_codes[:, 0 : 3 * P].bitcast(I32))
-        nc.sync.dma_start(out=y_words[:, 3 * P : N], in_=y_codes[:, 3 * P : N].bitcast(I32))
+        store_result(2)
+        z_bf[LAST] = sbuf([P, P, PLANES], BF16, "z_bf%d" % LAST)
+        nc.vector.tensor_copy(out=z_bf[LAST][:], in_=z_last[:].rearrange("p t v -> p v t"))
+        quantize_z(LAST)
+        second_layer(LAST, (3, 0))
+
+        y_codes = sbuf([P, N], U32, "y_codes", after="z_bf%d" % LAST)
+        halves = (slice(0, N // 2), slice(N // 2, N))
+
+        def quantize_result(cols):
+            quantize(y_codes[:, cols], y_scale[:, cols], y_bf[:, cols, :].rearrange("p v t -> p (v t)"))
+
+        quantize_result(halves[0])
+        round_result(2, nc.vector, y[2])
+        store_result(LAST)
+        round_result(LAST, nc.vector, y[LAST])
+        quantize_result(halves[1])
+        for cols in halves:
+            nc.sync.dma_start(out=y_words[:, cols], in_=y_codes[:, cols].bitcast(I32))
         for q in range(4):
             queue = nc.scalar if q % 2 else nc.sync
             queue.dma_start(
                 out=out_2[0, 4 * q : 4 * q + 4, :].bitcast(I32),
-                in_=y_scale[:].bitcast(I32)[32 * q : 32 * q + 4, :],
+                in_=y_scale[:].bitcast(I32)[QUADRANT * q : QUADRANT * q + 4, :],
             )

@@ -21,11 +21,11 @@ N = 512
 QUADRANT = 32
 LISTS = 2
 PER_COLUMN = 16
+RUN = 8
+BLOCKS = 16
 LAST = 3
-EARLY = 2
+SUMS = {0: (4, 4), 1: (4, 5), 2: (4, 7)}
 FLOPS = 2 * 2 * N * N * N
-
-PARTS = {0: ((0, 4, 4),), 1: ((0, 4, 5),), 2: ((0, 2, 6), (2, 4, 5))}
 
 
 def tile_picked_wlapl_gelu_lo_kernel(
@@ -53,21 +53,27 @@ def tile_picked_wlapl_gelu_lo_kernel(
 
         gate_rows = sbuf([P, LISTS, 4], F32, "gate_rows")
         nc.sync.dma_start(out=gate_rows[:], in_=gate[:, 0, :].rearrange("d (n j) -> n d j", j=4))
+        w1_raw = sbuf([P, PLANES, N], F32, "w1_raw")
+        nc.sync.dma_start(out=w1_raw[:], in_=w1.rearrange("(p j) i -> p j i", j=PLANES))
         x_scale = sbuf([P, N], U8, "x_scale")
-        for q in range(4):
-            nc.scalar.dma_start(
+
+        def load_scale_rows(queue, q):
+            queue.dma_start(
                 out=x_scale[:].bitcast(I32)[QUADRANT * q : QUADRANT * q + 4, :],
                 in_=x_scales[0, 4 * q : 4 * q + 4, :].bitcast(I32),
             )
-        w1_raw = sbuf([P, PLANES, N], F32, "w1_raw")
+
+        for q in range(4):
+            load_scale_rows(nc.scalar, q)
         x_codes = sbuf([P, N], U32, "x_codes")
         lists = [keep.tile([P, N // PER_COLUMN], U16, name="list%d" % d) for d in range(LISTS)]
         w2_raw = sbuf([P, PLANES, N], F32, "w2_raw")
-        nc.sync.dma_start(out=w1_raw[:], in_=w1.rearrange("(p j) i -> p j i", j=PLANES))
         nc.sync.dma_start(out=x_codes[:].bitcast(I32), in_=x_words[0].rearrange("p n t -> p (n t)").bitcast(I32))
         nc.sync.dma_start(lists[0][:], pos1)
         nc.sync.dma_start(lists[1][:], pos2)
-        nc.sync.dma_start(out=w2_raw[:], in_=w2.rearrange("(p j) m -> p j m", j=PLANES))
+        w2_rows = w2.rearrange("(q t r) m -> t q r m", t=PLANES, r=RUN)
+        for t in range(PLANES):
+            nc.sync.dma_start(out=w2_raw[:, t, :], in_=w2_rows[t])
 
         ident = sbuf([P, P], F32, "ident")
         ones = sbuf([P, P], F32, "ones")
@@ -98,13 +104,6 @@ def tile_picked_wlapl_gelu_lo_kernel(
                 scale=-1.0,
             )
 
-        def round_weights(engine, rounded, raw, t0, count):
-            copy(
-                engine,
-                out=rounded.rearrange("p t c j -> p c t j"),
-                in_=raw[:].rearrange("p j (c t) -> p c t j", t=PLANES)[:, :, t0 : t0 + count],
-            )
-
         def quantize(codes, scale, rounded):
             nc.vector.quantize_mx(out=codes.bitcast(FP8X4), scales=scale, in_=rounded)
 
@@ -116,16 +115,19 @@ def tile_picked_wlapl_gelu_lo_kernel(
 
         w1_bf, w1_mx, h = {}, {}, {}
 
-        def round_w1(t0, count, engine):
-            w1_bf[t0] = sbuf([P, count, P, PLANES], BF16, "w1_bf%d" % t0)
-            round_weights(engine, w1_bf[t0][:], w1_raw, t0, count)
+        def round_w1(t, engine, after=None):
+            w1_bf[t] = sbuf([P, P, PLANES], BF16, "w1_bf%d" % t, after)
+            copy(
+                engine,
+                out=w1_bf[t][:].rearrange("p (q r) j -> p q r j", r=RUN),
+                in_=w1_raw[:].rearrange("p j (q t r) -> p t q r j", t=PLANES, r=RUN)[:, t],
+            )
 
-        def quantize_w1(t0, count):
-            codes = sbuf([P, count * P], U32, "w1_codes%d" % t0)
-            scale = sbuf([P, count * P], U8, "w1_scale%d" % t0)
-            quantize(codes[:], scale[:], w1_bf[t0][:].rearrange("p t c j -> p (t c j)"))
-            for t in range(count):
-                w1_mx[t0 + t] = codes[:, block(t)], scale[:, block(t)]
+        def quantize_w1(t):
+            codes = sbuf([P, P], U32, "w1_codes%d" % t)
+            scale = sbuf([P, P], U8, "w1_scale%d" % t)
+            quantize(codes[:], scale[:], w1_bf[t][:].rearrange("p c j -> p (c j)"))
+            w1_mx[t] = codes[:], scale[:]
 
         def first_layer(t, bank_numbers):
             h[t] = sbuf([P, N], F32, "h%d" % t)
@@ -136,19 +138,19 @@ def tile_picked_wlapl_gelu_lo_kernel(
                 product(pre[:], w1_mx[t][0], w1_mx[t][1], x_codes[:, nodes], x_scale[:, nodes])
                 nc.scalar.activation(h[t][:, nodes], pre[:], GELU)
 
-        zt, zt_bf, z_bf = {}, {}, {}
+        zt, z_bf = {}, {}
 
         def gather(term, t, d, v0, v1):
             window = h[t][:].indirect(lists[d][:, v0 // PER_COLUMN : v1 // PER_COLUMN])
             nc.vector.tensor_tensor(term, window, neg_gate[d][:, v0:v1], MULT)
 
         def add_turned(b, t, src, own, last):
-            t0, t1, bank = [part for part in PARTS[b] if part[0] <= t < part[1]][0]
-            if own and t == t0:
-                zt[b, t0] = psum([P, (t1 - t0) * P], "zt%d_%d" % (b, t0), bank)
+            count, bank = SUMS[b]
+            if own and t == 0:
+                zt[b] = psum([P, count * P], "zt%d" % b, bank)
             nc.tensor.matmul(
-                zt[b, t0][:, block(t - t0)], lhsT=src, rhs=ident[:], is_transpose=True,
-                start=own and t == t0, stop=last and t == t1 - 1,
+                zt[b][:, block(t)], lhsT=src, rhs=ident[:], is_transpose=True,
+                start=own and t == 0, stop=last and t == count - 1,
             )
 
         def sum_by_transposes(blocks, t, terms):
@@ -159,30 +161,29 @@ def tile_picked_wlapl_gelu_lo_kernel(
                 for n, b in enumerate(blocks):
                     add_turned(b, t, terms[:, d, block(n)], False, d == LISTS - 1)
 
-        def round_turned(b, after=None):
-            zt_bf[b] = sbuf([P, 2, P, 2], BF16, "zt_bf%d" % b, after)
-            for t0, t1, bank in PARTS[b]:
-                nc.scalar.copy(
-                    out=zt_bf[b][:, t0 // 2 : t1 // 2],
-                    in_=zt[b, t0][:].rearrange("v (u e p) -> v u p e", e=2, p=P),
-                )
-
-        def turn_back(b, bank):
-            pairs = zt_bf[b][:].rearrange("v u p e -> v (u p e)").bitcast(F32)
-            back = psum([P, 2, P], "back%d" % b, bank)
-            for u in range(2):
-                nc.tensor.transpose(back[:, u, :], pairs[:, block(u)], ident[:])
-            z_bf[b] = sbuf([P, P, PLANES], BF16, "z_bf%d" % b)
+        def turn_back(b, bank, rounded):
+            halves = SUMS[b][0] // 2
             nc.scalar.copy(
-                out=z_bf[b][:].rearrange("p v t -> p (v t)").bitcast(F32).rearrange("p (v u) -> p v u", u=2),
-                in_=back[:].rearrange("p u v -> p v u"),
+                out=rounded.rearrange("v (u p e) -> v u p e", e=2, p=P),
+                in_=zt[b][:].rearrange("v (u e p) -> v u p e", e=2, p=P),
             )
+            pairs = rounded.bitcast(F32)
+            back = psum([P, halves, P], "back%d" % b, bank)
+            for u in range(halves):
+                nc.tensor.transpose(back[:, u, :], pairs[:, block(u)], ident[:])
+            return back
+
+        def as_pairs(tile):
+            return tile[:].rearrange("p v t -> p (v t)").bitcast(F32).rearrange("p (v u) -> p v u", u=2)
+
+        def weave(b, back):
+            z_bf[b] = sbuf([P, P, PLANES], BF16, "z_bf%d" % b)
+            nc.scalar.copy(out=as_pairs(z_bf[b]), in_=back[:].rearrange("p u v -> p v u"))
 
         w2_bf = sbuf([P, PLANES, P, PLANES], BF16, "w2_bf")
         w2_codes = sbuf([P, N], U32, "w2_codes")
         w2_scale = sbuf([P, N], U8, "w2_scale")
-        y = [sbuf([P, PLANES, P], F32, "y%d" % b) for b in range(N // P)]
-        y_bf = sbuf([P, N, PLANES], BF16, "y_bf")
+        y = [sbuf([P, PLANES, P], F32, "y%d" % b)[:] for b in range(N // P)]
         y_scale = sbuf([P, N], U8, "y_scale")
         y_rows = out_0.rearrange("(p t) v -> p t v", t=PLANES)
         y_words = out_1[0].rearrange("p n t -> p (n t)").bitcast(I32)
@@ -207,78 +208,103 @@ def tile_picked_wlapl_gelu_lo_kernel(
             per_bank = PLANES // len(acc[b])
             for n, sums in enumerate(acc[b]):
                 nc.scalar.copy(out=y[b][:, n * per_bank : (n + 1) * per_bank, :], in_=sums[:])
-            nc.sync.dma_start(out=y_rows[:, :, block(b)], in_=y[b][:])
+            nc.sync.dma_start(out=y_rows[:, :, block(b)], in_=y[b])
 
-        def round_result(b, engine, src):
-            copy(engine, out=y_bf[:, block(b), :], in_=src[:].rearrange("p t v -> p v t"))
+        def round_result(rounded, engine, src):
+            copy(engine, out=rounded.rearrange("p (v t) -> p v t", t=PLANES), in_=src[:].rearrange("p t v -> p v t"))
 
-        round_w1(0, 1, nc.vector)
-        round_w1(2, 2, nc.scalar)
-        quantize_w1(0, 1)
-        first_layer(0, (2, 7))
-        round_w1(1, 1, nc.vector)
-        quantize_w1(1, 1)
-        first_layer(1, (3,))
-        quantize_w1(2, 2)
-        first_layer(2, (0,))
-        first_layer(3, (1,))
+        def quantize_result(b, rounded, after=None):
+            width = rounded.shape[1] // PLANES
+            cols = slice(b * P, b * P + width)
+            codes = sbuf([P, width], U32, "y_codes%d" % b, after)
+            quantize(codes[:], y_scale[:, cols], rounded)
+            nc.sync.dma_start(out=y_words[:, cols], in_=codes[:].bitcast(I32))
 
-        for t in range(PLANES):
+        round_w1(0, nc.vector)
+        round_w1(1, nc.scalar)
+        round_w1(2, nc.scalar)
+        quantize_w1(0)
+        first_layer(0, (0, 1))
+        quantize_w1(1)
+        first_layer(1, (2,))
+        quantize_w1(2)
+        first_layer(2, (3,))
+        round_w1(3, nc.vector, after="w1_bf0")
+        quantize_w1(3)
+        first_layer(3, (6,))
+
+        def terms_for(name, count, after=None):
+            return sbuf([P, count, LISTS, P], F32, name, after)
+
+        for t in range(PLANES - 1):
             sum_by_transposes((0, 1), t, sbuf([P, LISTS, 2 * P], F32, "terms01_%d" % t))
-        for t0 in (0, 2):
-            round_weights(nc.scalar, w2_bf[:, t0 : t0 + 2], w2_raw, t0, 2)
-        terms2 = sbuf([P, PLANES, LISTS, P], F32, "terms2", after="terms01_1")
-        round_turned(0)
-        round_turned(1)
-        turn_back(0, 2)
-        turn_back(1, 7)
-        for t in range(PLANES):
-            sum_by_transposes((2,), t, terms2[:, t])
-        quantize(w2_codes[:], w2_scale[:], w2_bf[:].rearrange("p t c j -> p (t c j)"))
-        quantize_z(0)
-        second_layer(0, (3,))
-        quantize_z(1)
-        round_turned(2, after="zt_bf1")
-        turn_back(2, 2)
-        second_layer(1, (5,))
         for b in range(2):
-            store_result(b)
-            round_result(b, nc.scalar, acc[b][0])
-
-        early = sbuf([P, EARLY, P], F32, "early", after="zt_bf0")
-        late = sbuf([P, LISTS * PLANES - EARLY, P], F32, "late", after="z_bf0")
+            sum_by_transposes((b,), PLANES - 1, terms_for("terms%d_3" % b, 1)[:, 0])
+        nc.scalar.copy(
+            out=w2_bf[:].rearrange("p t c j -> p c t j"),
+            in_=w2_raw[:].rearrange("p j (c t) -> p c t j", t=PLANES),
+        )
+        stage = sbuf([P, N + 3 * LISTS * P], F32, "stage", after="w2_raw")
+        back0 = turn_back(0, 1, stage[:, 0 : N // 2].bitcast(BF16))
+        back1 = turn_back(1, 2, stage[:, N // 2 : N].bitcast(BF16))
+        weave(0, back0)
+        weave(1, back1)
+        terms = terms_for("terms2", 1, after="terms01_1")
+        for t in range(1):
+            sum_by_transposes((2,), t, terms[:, t])
+        quantize(w2_codes[:], w2_scale[:], w2_bf[:].rearrange("p t c j -> p (t c j)"))
+        terms = stage[:, N:].rearrange("p (t d v) -> p t d v", d=LISTS, v=P)
+        for t in range(3):
+            sum_by_transposes((2,), 1 + t, terms[:, t])
+        quantize_z(0)
+        second_layer(0, (4,))
+        quantize_z(1)
+        back2 = turn_back(2, 3, sbuf([P, N], BF16, "zt_bf2")[:])
+        second_layer(1, (7,))
+        store_result(0)
+        weave(2, back2)
+        store_result(1)
+        terms = sbuf([P, 6, P], F32, "terms3", after="w2_bf")
         with_first = sbuf([P, PLANES, P], F32, "with_first")
-        z_last = sbuf([P, PLANES, P], F32, "z_last")
-        second = late[:, PLANES - EARLY :, :]
+        late = sbuf([P, 2 * N], F32, "late", after="zt_bf2")
+        pair_words = late[:, 0 : 2 * P].rearrange("p (u v) -> p u v", u=2)
+        second = [terms[:, 4:6], late[:, 2 * P : N].rearrange("p (e v) -> p e v", e=2)]
+
+        def add_pair(u):
+            nc.vector.tensor_tensor(
+                pair_words[:, u].bitcast(BF16).rearrange("p (v e) -> p v e", e=2),
+                with_first[:, 2 * u : 2 * u + 2].rearrange("p e v -> p v e"),
+                second[u].rearrange("p e v -> p v e"), ADD,
+            )
+
         for t in range(PLANES):
-            term = early[:, t, :] if t < EARLY else late[:, t - EARLY, :]
-            gather(term, t, 0, LAST * P, N)
-            nc.vector.tensor_tensor(with_first[:, t, :], h[t][:, block(LAST)], term, ADD)
+            gather(terms[:, t, :], t, 0, LAST * P, N)
         for t in range(PLANES):
-            gather(second[:, t, :], t, 1, LAST * P, N)
-        for planes in (slice(0, PLANES - 1), slice(PLANES - 1, PLANES)):
-            nc.vector.tensor_tensor(z_last[:, planes, :], with_first[:, planes, :], second[:, planes, :], ADD)
+            if t < 2:
+                gather(second[0][:, t, :], t, 1, LAST * P, N)
+            nc.vector.tensor_tensor(with_first[:, t, :], h[t][:, block(LAST)], terms[:, t, :], ADD)
         quantize_z(2)
-        second_layer(2, (1,))
+        second_layer(2, (5,))
+        gather(second[1][:, 0, :], 2, 1, LAST * P, N)
+        add_pair(0)
+        gather(second[1][:, 1, :], 3, 1, LAST * P, N)
+        y_bf01 = late[:, N : 2 * N].bitcast(BF16)
+        for b in range(2):
+            round_result(y_bf01[:, b * N : (b + 1) * N], nc.scalar, acc[b][0])
         store_result(2)
+        add_pair(1)
         z_bf[LAST] = sbuf([P, P, PLANES], BF16, "z_bf%d" % LAST)
-        nc.vector.tensor_copy(out=z_bf[LAST][:], in_=z_last[:].rearrange("p t v -> p v t"))
+        nc.vector.tensor_copy(out=as_pairs(z_bf[LAST]), in_=pair_words.rearrange("p u v -> p v u"))
         quantize_z(LAST)
-        second_layer(LAST, (3, 0))
-
-        y_codes = sbuf([P, N], U32, "y_codes", after="z_bf%d" % LAST)
-        halves = (slice(0, N // 2), slice(N // 2, N))
-
-        def quantize_result(cols):
-            quantize(y_codes[:, cols], y_scale[:, cols], y_bf[:, cols, :].rearrange("p v t -> p (v t)"))
-
-        quantize_result(halves[0])
-        round_result(2, nc.vector, y[2])
+        second_layer(LAST, (1, 2))
+        quantize_result(0, y_bf01, after="z_bf%d" % LAST)
+        y_bf2 = sbuf([P, N], BF16, "y_bf2")
+        round_result(y_bf2[:], nc.vector, y[2])
+        quantize_result(2, y_bf2[:])
         store_result(LAST)
-        round_result(LAST, nc.vector, y[LAST])
-        quantize_result(halves[1])
-        for cols in halves:
-            nc.sync.dma_start(out=y_words[:, cols], in_=y_codes[:, cols].bitcast(I32))
+        y_bf3 = sbuf([P, N], BF16, "y_bf3")
+        round_result(y_bf3[:], nc.vector, y[LAST])
+        quantize_result(3, y_bf3[:])
         for q in range(4):
             queue = nc.scalar if q % 2 else nc.sync
             queue.dma_start(

@@ -21,6 +21,7 @@ N = 512
 QUADRANT = 32
 LISTS = 2
 PER_COLUMN = 16
+LINE = 4
 RUN = 8
 BLOCKS = 16
 LAST = 3
@@ -34,10 +35,14 @@ def tile_picked_wlapl_gelu_lo_kernel(
     nc = tc.nc
     with ExitStack() as ctx:
         keep = ctx.enter_context(tc.tile_pool(name="keep", bufs=1))
+        shared = ctx.enter_context(tc.tile_pool(name="shared", bufs=1))
         banks = ctx.enter_context(tc.psum_pool(name="banks", bufs=1))
 
         def sbuf(shape, dtype, name, after=None):
             return keep.tile(shape, dtype, name=name, tag=after or name, align_bytes=64)
+
+        def placed(shape, dtype, name, offset):
+            return shared.tile(shape, dtype, name=name, align_bytes=64, offset=offset)
 
         def psum(shape, name, bank):
             return banks.tile(shape, F32, name=name, tag="bank%d" % bank)
@@ -67,7 +72,7 @@ def tile_picked_wlapl_gelu_lo_kernel(
             load_scale_rows(nc.scalar, q)
         x_codes = sbuf([P, N], U32, "x_codes")
         lists = [keep.tile([P, N // PER_COLUMN], U16, name="list%d" % d) for d in range(LISTS)]
-        w2_raw = sbuf([P, PLANES, N], F32, "w2_raw")
+        w2_raw = placed([P, PLANES, N], F32, "w2_raw", 0)
         nc.sync.dma_start(out=x_codes[:].bitcast(I32), in_=x_words[0].rearrange("p n t -> p (n t)").bitcast(I32))
         nc.sync.dma_start(lists[0][:], pos1)
         nc.sync.dma_start(lists[1][:], pos2)
@@ -119,8 +124,8 @@ def tile_picked_wlapl_gelu_lo_kernel(
             w1_bf[t] = sbuf([P, P, PLANES], BF16, "w1_bf%d" % t, after)
             copy(
                 engine,
-                out=w1_bf[t][:].rearrange("p (q r) j -> p q r j", r=RUN),
-                in_=w1_raw[:].rearrange("p j (q t r) -> p t q r j", t=PLANES, r=RUN)[:, t],
+                out=w1_bf[t][:].rearrange("p (q a i) j -> p q a j i", a=RUN // LINE, i=LINE),
+                in_=w1_raw[:].rearrange("p j (q t a i) -> p t q a j i", t=PLANES, a=RUN // LINE, i=LINE)[:, t],
             )
 
         def quantize_w1(t):
@@ -211,14 +216,11 @@ def tile_picked_wlapl_gelu_lo_kernel(
             nc.sync.dma_start(out=y_rows[:, :, block(b)], in_=y[b])
 
         def round_result(rounded, engine, src):
-            copy(engine, out=rounded.rearrange("p (v t) -> p v t", t=PLANES), in_=src[:].rearrange("p t v -> p v t"))
-
-        def quantize_result(b, rounded, after=None):
-            width = rounded.shape[1] // PLANES
-            cols = slice(b * P, b * P + width)
-            codes = sbuf([P, width], U32, "y_codes%d" % b, after)
-            quantize(codes[:], y_scale[:, cols], rounded)
-            nc.sync.dma_start(out=y_words[:, cols], in_=codes[:].bitcast(I32))
+            copy(
+                engine,
+                out=rounded.rearrange("p (c i t) -> p c t i", i=LINE, t=PLANES),
+                in_=src[:].rearrange("p t (c i) -> p c t i", i=LINE),
+            )
 
         round_w1(0, nc.vector)
         round_w1(1, nc.scalar)
@@ -244,16 +246,16 @@ def tile_picked_wlapl_gelu_lo_kernel(
             out=w2_bf[:].rearrange("p t c j -> p c t j"),
             in_=w2_raw[:].rearrange("p j (c t) -> p c t j", t=PLANES),
         )
-        stage = sbuf([P, N + 3 * LISTS * P], F32, "stage", after="w2_raw")
-        back0 = turn_back(0, 1, stage[:, 0 : N // 2].bitcast(BF16))
-        back1 = turn_back(1, 2, stage[:, N // 2 : N].bitcast(BF16))
+        zt_bf01 = placed([P, 2 * N], BF16, "zt_bf01", 0)
+        back0 = turn_back(0, 1, zt_bf01[:, 0:N])
+        back1 = turn_back(1, 2, zt_bf01[:, N : 2 * N])
         weave(0, back0)
         weave(1, back1)
         terms = terms_for("terms2", 1, after="terms01_1")
         for t in range(1):
             sum_by_transposes((2,), t, terms[:, t])
         quantize(w2_codes[:], w2_scale[:], w2_bf[:].rearrange("p t c j -> p (t c j)"))
-        terms = stage[:, N:].rearrange("p (t d v) -> p t d v", d=LISTS, v=P)
+        terms = placed([P, 3, LISTS, P], F32, "terms2_late", 4096)
         for t in range(3):
             sum_by_transposes((2,), 1 + t, terms[:, t])
         quantize_z(0)
@@ -264,47 +266,40 @@ def tile_picked_wlapl_gelu_lo_kernel(
         store_result(0)
         weave(2, back2)
         store_result(1)
-        terms = sbuf([P, 6, P], F32, "terms3", after="w2_bf")
-        with_first = sbuf([P, PLANES, P], F32, "with_first")
+        terms = placed([P, LISTS, PLANES, P], F32, "terms3", 0)
         late = sbuf([P, 2 * N], F32, "late", after="zt_bf2")
-        pair_words = late[:, 0 : 2 * P].rearrange("p (u v) -> p u v", u=2)
-        second = [terms[:, 4:6], late[:, 2 * P : N].rearrange("p (e v) -> p e v", e=2)]
+        with_first = late[:, 0:N].rearrange("p (t v) -> p t v", t=PLANES)
 
-        def add_pair(u):
-            nc.vector.tensor_tensor(
-                pair_words[:, u].bitcast(BF16).rearrange("p (v e) -> p v e", e=2),
-                with_first[:, 2 * u : 2 * u + 2].rearrange("p e v -> p v e"),
-                second[u].rearrange("p e v -> p v e"), ADD,
-            )
-
-        for t in range(PLANES):
-            gather(terms[:, t, :], t, 0, LAST * P, N)
-        for t in range(PLANES):
-            if t < 2:
-                gather(second[0][:, t, :], t, 1, LAST * P, N)
-            nc.vector.tensor_tensor(with_first[:, t, :], h[t][:, block(LAST)], terms[:, t, :], ADD)
+        for d in range(LISTS):
+            for t in range(PLANES):
+                gather(terms[:, d, t, :], t, d, LAST * P, N)
         quantize_z(2)
         second_layer(2, (5,))
-        gather(second[1][:, 0, :], 2, 1, LAST * P, N)
-        add_pair(0)
-        gather(second[1][:, 1, :], 3, 1, LAST * P, N)
+        for t in range(PLANES):
+            nc.vector.tensor_tensor(with_first[:, t, :], h[t][:, block(LAST)], terms[:, 0, t, :], ADD)
         y_bf01 = late[:, N : 2 * N].bitcast(BF16)
         for b in range(2):
             round_result(y_bf01[:, b * N : (b + 1) * N], nc.scalar, acc[b][0])
         store_result(2)
-        add_pair(1)
         z_bf[LAST] = sbuf([P, P, PLANES], BF16, "z_bf%d" % LAST)
-        nc.vector.tensor_copy(out=as_pairs(z_bf[LAST]), in_=pair_words.rearrange("p u v -> p v u"))
+        nc.vector.tensor_tensor(
+            z_bf[LAST][:].rearrange("p (c i) t -> p c t i", i=LINE),
+            with_first.rearrange("p t (c i) -> p c t i", i=LINE),
+            terms[:, 1].rearrange("p t (c i) -> p c t i", i=LINE), ADD,
+        )
         quantize_z(LAST)
         second_layer(LAST, (1, 2))
-        quantize_result(0, y_bf01, after="z_bf%d" % LAST)
-        y_bf2 = sbuf([P, N], BF16, "y_bf2")
-        round_result(y_bf2[:], nc.vector, y[2])
-        quantize_result(2, y_bf2[:])
-        store_result(LAST)
-        y_bf3 = sbuf([P, N], BF16, "y_bf3")
-        round_result(y_bf3[:], nc.vector, y[LAST])
-        quantize_result(3, y_bf3[:])
+        y_codes = sbuf([P, N], U32, "y_codes")
+        for b in range(2):
+            quantize(y_codes[:, block(b)], y_scale[:, block(b)], y_bf01[:, b * N : (b + 1) * N])
+            nc.sync.dma_start(out=y_words[:, block(b)], in_=y_codes[:, block(b)].bitcast(I32))
+        for b in (2, LAST):
+            if b == LAST:
+                store_result(LAST)
+            y_bf = sbuf([P, N], BF16, "y_bf%d" % b)
+            round_result(y_bf[:], nc.vector, y[b])
+            quantize(y_codes[:, block(b)], y_scale[:, block(b)], y_bf[:])
+        nc.sync.dma_start(out=y_words[:, 2 * P : N], in_=y_codes[:, 2 * P : N].bitcast(I32))
         for q in range(4):
             queue = nc.scalar if q % 2 else nc.sync
             queue.dma_start(

@@ -56,8 +56,9 @@ def tile_picked_wlapl_gelu_lo_kernel(
         def block(b):
             return slice(b * P, (b + 1) * P)
 
-        gate_rows = sbuf([P, LISTS, 4], F32, "gate_rows")
-        nc.sync.dma_start(out=gate_rows[:], in_=gate[:, 0, :].rearrange("d (n j) -> n d j", j=4))
+        gate_rows = sbuf([P, 8], F32, "gate_rows")
+        gate_run = gate.rearrange("d r v -> (d r) v")[P - 1 : P + 1, :]
+        nc.sync.dma_start(out=gate_rows[:], in_=gate_run.rearrange("d (n j) -> (d n) j", j=8))
         w1_raw = sbuf([P, PLANES, N], F32, "w1_raw")
         nc.sync.dma_start(out=w1_raw[:], in_=w1.rearrange("(p j) i -> p j i", j=PLANES))
         x_scale = sbuf([P, N], U8, "x_scale")
@@ -96,15 +97,15 @@ def tile_picked_wlapl_gelu_lo_kernel(
         nc.vector.tensor_tensor(row[:], in_quadrant[:, 0:1], quadrant_start[:], ADD)
         nc.vector.tensor_scalar(ident[:], column[:], row[:, 0:1], None, IS_EQUAL)
 
-        gate_banks = [psum([P, 4, P], "gate_bank%d" % d, 4 + d) for d in range(LISTS)]
-        for d in range(LISTS):
+        neg_gate = sbuf([P, LISTS, N], F32, "neg_gate")
+        for half in range(2):
+            spread = psum([P, 4, P], "gate_bank%d" % half, 4 + half)
             for j in range(4):
-                nc.tensor.transpose(gate_banks[d][:, j, :], gate_rows[:, d, j : j + 1].to_broadcast([P, P]), ident[:])
-        neg_gate = [sbuf([P, N], F32, "neg_gate%d" % d) for d in range(LISTS)]
-        for d in range(LISTS):
+                col = 4 * half + j
+                nc.tensor.transpose(spread[:, j, :], gate_rows[:, col : col + 1].to_broadcast([P, P]), ident[:])
             nc.scalar.activation(
-                neg_gate[d][:].rearrange("p (n j) -> p n j", j=4),
-                gate_banks[d][:].rearrange("p j n -> p n j"),
+                neg_gate[:].rearrange("p d (n a j) -> p a (d n) j", a=2, j=4)[:, half],
+                spread[:].rearrange("p j q -> p q j"),
                 COPY,
                 scale=-1.0,
             )
@@ -120,8 +121,8 @@ def tile_picked_wlapl_gelu_lo_kernel(
 
         w1_bf, w1_mx, h = {}, {}, {}
 
-        def round_w1(t, engine, after=None):
-            w1_bf[t] = sbuf([P, P, PLANES], BF16, "w1_bf%d" % t, after)
+        def round_w1(t, engine, rounded):
+            w1_bf[t] = rounded
             copy(
                 engine,
                 out=w1_bf[t][:].rearrange("p (q a i) j -> p q a j i", a=RUN // LINE, i=LINE),
@@ -147,7 +148,7 @@ def tile_picked_wlapl_gelu_lo_kernel(
 
         def gather(term, t, d, v0, v1):
             window = h[t][:].indirect(lists[d][:, v0 // PER_COLUMN : v1 // PER_COLUMN])
-            nc.vector.tensor_tensor(term, window, neg_gate[d][:, v0:v1], MULT)
+            nc.vector.tensor_tensor(term, window, neg_gate[:, d, v0:v1], MULT)
 
         def add_turned(b, t, src, own, last):
             count, bank = SUMS[b]
@@ -222,18 +223,18 @@ def tile_picked_wlapl_gelu_lo_kernel(
                 in_=src[:].rearrange("p t (c i) -> p c t i", i=LINE),
             )
 
-        round_w1(0, nc.vector)
-        round_w1(1, nc.scalar)
-        round_w1(2, nc.scalar)
+        round_w1(0, nc.vector, sbuf([P, P, PLANES], BF16, "w1_bf0")[:])
+        round_w1(1, nc.scalar, sbuf([P, P, PLANES], BF16, "w1_bf1")[:])
         quantize_w1(0)
-        first_layer(0, (0, 1))
+        first_layer(0, (0, 1, 7, 4))
         quantize_w1(1)
         first_layer(1, (2,))
-        quantize_w1(2)
-        first_layer(2, (3,))
-        round_w1(3, nc.vector, after="w1_bf0")
-        quantize_w1(3)
-        first_layer(3, (6,))
+        w1_bf23 = sbuf([P, 2 * N], BF16, "w1_bf23", after="w1_bf0")
+        for t, bank in ((2, 3), (3, 6)):
+            rounded = w1_bf23[:, (t - 2) * N : (t - 1) * N]
+            round_w1(t, nc.vector, rounded.rearrange("p (c j) -> p c j", j=PLANES))
+            quantize_w1(t)
+            first_layer(t, (bank,))
 
         def terms_for(name, count, after=None):
             return sbuf([P, count, LISTS, P], F32, name, after)
@@ -274,7 +275,7 @@ def tile_picked_wlapl_gelu_lo_kernel(
             for t in range(PLANES):
                 gather(terms[:, d, t, :], t, d, LAST * P, N)
         quantize_z(2)
-        second_layer(2, (5,))
+        second_layer(2, (5, 0))
         for t in range(PLANES):
             nc.vector.tensor_tensor(with_first[:, t, :], h[t][:, block(LAST)], terms[:, 0, t, :], ADD)
         y_bf01 = late[:, N : 2 * N].bitcast(BF16)
@@ -288,7 +289,7 @@ def tile_picked_wlapl_gelu_lo_kernel(
             terms[:, 1].rearrange("p t (c i) -> p c t i", i=LINE), ADD,
         )
         quantize_z(LAST)
-        second_layer(LAST, (1, 2))
+        second_layer(LAST, (1, 2, 3, 6))
         y_codes = sbuf([P, N], U32, "y_codes")
         for b in range(2):
             quantize(y_codes[:, block(b)], y_scale[:, block(b)], y_bf01[:, b * N : (b + 1) * N])

@@ -70,7 +70,7 @@ def tile_picked_wlapl_gelu_lo_kernel(
             )
 
         for q in range(4):
-            load_scale_rows(nc.scalar, q)
+            load_scale_rows(nc.scalar if q % 2 else nc.sync, q)
         x_codes = sbuf([P, N], U32, "x_codes")
         lists = [keep.tile([P, N // PER_COLUMN], U16, name="list%d" % d) for d in range(LISTS)]
         w2_raw = placed([P, PLANES, N], F32, "w2_raw", 0)
@@ -103,12 +103,11 @@ def tile_picked_wlapl_gelu_lo_kernel(
             for j in range(4):
                 col = 4 * half + j
                 nc.tensor.transpose(spread[:, j, :], gate_rows[:, col : col + 1].to_broadcast([P, P]), ident[:])
-            nc.scalar.activation(
-                neg_gate[:].rearrange("p d (n a j) -> p a (d n) j", a=2, j=4)[:, half],
-                spread[:].rearrange("p j q -> p q j"),
-                COPY,
-                scale=-1.0,
-            )
+            negated = neg_gate[:].rearrange("p d (n a j) -> p a (d n) j", a=2, j=4)[:, half]
+            if half == 1:
+                nc.scalar.activation(negated, spread[:].rearrange("p j q -> p q j"), COPY, scale=-1.0)
+            else:
+                nc.vector.tensor_scalar(negated, spread[:].rearrange("p j q -> p q j"), -1.0, None, MULT)
 
         def quantize(codes, scale, rounded):
             nc.vector.quantize_mx(out=codes.bitcast(FP8X4), scales=scale, in_=rounded)
@@ -121,18 +120,22 @@ def tile_picked_wlapl_gelu_lo_kernel(
 
         w1_bf, w1_mx, h = {}, {}, {}
 
-        def round_w1(t, engine, rounded):
+        def round_w1(t, engine, rounded, parts=1):
             w1_bf[t] = rounded
-            copy(
-                engine,
-                out=w1_bf[t][:].rearrange("p (q a i) j -> p q a j i", a=RUN // LINE, i=LINE),
-                in_=w1_raw[:].rearrange("p j (q t a i) -> p t q a j i", t=PLANES, a=RUN // LINE, i=LINE)[:, t],
-            )
+            for n in range(parts):
+                runs = slice(n * BLOCKS // parts, (n + 1) * BLOCKS // parts)
+                copy(
+                    engine,
+                    out=w1_bf[t][:].rearrange("p (q a i) j -> p q a j i", a=RUN // LINE, i=LINE)[:, runs],
+                    in_=w1_raw[:].rearrange("p j (q t a i) -> p t q a j i", t=PLANES, a=RUN // LINE, i=LINE)[:, t, runs],
+                )
 
-        def quantize_w1(t):
+        def quantize_w1(t, parts=1):
             codes = sbuf([P, P], U32, "w1_codes%d" % t)
             scale = sbuf([P, P], U8, "w1_scale%d" % t)
-            quantize(codes[:], scale[:], w1_bf[t][:].rearrange("p c j -> p (c j)"))
+            for n in range(parts):
+                cols = slice(n * P // parts, (n + 1) * P // parts)
+                quantize(codes[:, cols], scale[:, cols], w1_bf[t][:, cols].rearrange("p c j -> p (c j)"))
             w1_mx[t] = codes[:], scale[:]
 
         def first_layer(t, bank_numbers):
@@ -223,9 +226,9 @@ def tile_picked_wlapl_gelu_lo_kernel(
                 in_=src[:].rearrange("p t (c i) -> p c t i", i=LINE),
             )
 
-        round_w1(0, nc.vector, sbuf([P, P, PLANES], BF16, "w1_bf0")[:])
+        round_w1(0, nc.vector, sbuf([P, P, PLANES], BF16, "w1_bf0")[:], parts=2)
         round_w1(1, nc.scalar, sbuf([P, P, PLANES], BF16, "w1_bf1")[:])
-        quantize_w1(0)
+        quantize_w1(0, parts=2)
         first_layer(0, (0, 1, 7, 4))
         quantize_w1(1)
         first_layer(1, (2,))
@@ -283,23 +286,31 @@ def tile_picked_wlapl_gelu_lo_kernel(
             round_result(y_bf01[:, b * N : (b + 1) * N], nc.scalar, acc[b][0])
         store_result(2)
         z_bf[LAST] = sbuf([P, P, PLANES], BF16, "z_bf%d" % LAST)
-        nc.vector.tensor_tensor(
-            z_bf[LAST][:].rearrange("p (c i) t -> p c t i", i=LINE),
-            with_first.rearrange("p t (c i) -> p c t i", i=LINE),
-            terms[:, 1].rearrange("p t (c i) -> p c t i", i=LINE), ADD,
-        )
-        quantize_z(LAST)
+        halves = [slice(n * P // 2, (n + 1) * P // 2) for n in range(2)]
+        for half in halves:
+            nc.vector.tensor_tensor(
+                z_bf[LAST][:, half].rearrange("p (c i) t -> p c t i", i=LINE),
+                with_first[:, :, half].rearrange("p t (c i) -> p c t i", i=LINE),
+                terms[:, 1, :, half].rearrange("p t (c i) -> p c t i", i=LINE), ADD,
+            )
+        z_mx[LAST] = sbuf([P, P], U32, "z_codes3"), sbuf([P, P], U8, "z_scale3")
+        for half in halves:
+            quantize(z_mx[LAST][0][:, half], z_mx[LAST][1][:, half], z_bf[LAST][:, half].rearrange("p v t -> p (v t)"))
         second_layer(LAST, (1, 2, 3, 6))
         y_codes = sbuf([P, N], U32, "y_codes")
         for b in range(2):
             quantize(y_codes[:, block(b)], y_scale[:, block(b)], y_bf01[:, b * N : (b + 1) * N])
-            nc.sync.dma_start(out=y_words[:, block(b)], in_=y_codes[:, block(b)].bitcast(I32))
-        for b in (2, LAST):
-            if b == LAST:
-                store_result(LAST)
-            y_bf = sbuf([P, N], BF16, "y_bf%d" % b)
-            round_result(y_bf[:], nc.vector, y[b])
-            quantize(y_codes[:, block(b)], y_scale[:, block(b)], y_bf[:])
+        nc.sync.dma_start(out=y_words[:, 0 : 2 * P], in_=y_codes[:, 0 : 2 * P].bitcast(I32))
+        y_bf2 = sbuf([P, N], BF16, "y_bf2")
+        round_result(y_bf2[:], nc.vector, y[2])
+        quantize(y_codes[:, block(2)], y_scale[:, block(2)], y_bf2[:])
+        store_result(LAST)
+        y_bf3 = [sbuf([P, N // 2], BF16, "y_bf3_%d" % n) for n in range(2)]
+        for n, half in enumerate(halves):
+            round_result(y_bf3[n][:], nc.vector, y[LAST][:, :, half])
+        for n, half in enumerate(halves):
+            cols = slice(LAST * P + half.start, LAST * P + half.stop)
+            quantize(y_codes[:, cols], y_scale[:, cols], y_bf3[n][:])
         nc.sync.dma_start(out=y_words[:, 2 * P : N], in_=y_codes[:, 2 * P : N].bitcast(I32))
         for q in range(4):
             queue = nc.scalar if q % 2 else nc.sync

@@ -304,7 +304,10 @@ def tile_picked_wlapl_gelu_lo_kernel(
         y_bf2 = sbuf([P, N], BF16, "y_bf2")
         round_result(y_bf2[:], nc.vector, y[2])
         quantize(y_codes[:, block(2)], y_scale[:, block(2)], y_bf2[:])
-        store_result(LAST)
+        for t, sums in enumerate(acc[LAST]):
+            nc.scalar.copy(out=y[LAST][:, t : t + 1, :], in_=sums[:])
+            if t % 2:
+                nc.sync.dma_start(out=y_rows[:, t - 1 : t + 1, block(LAST)], in_=y[LAST][:, t - 1 : t + 1, :])
         y_bf3 = [sbuf([P, N // 2], BF16, "y_bf3_%d" % n) for n in range(2)]
         for n, half in enumerate(halves):
             round_result(y_bf3[n][:], nc.vector, y[LAST][:, :, half])

@@ -253,8 +253,11 @@ def tile_picked_wlapl_gelu_lo_kernel(
         zt_bf01 = placed([P, 2 * N], BF16, "zt_bf01", 0)
         back0 = turn_back(0, 1, zt_bf01[:, 0:N])
         back1 = turn_back(1, 2, zt_bf01[:, N : 2 * N])
-        weave(0, back0)
-        weave(1, back1)
+        second = placed([P, PLANES, P], F32, "second", 2048)
+        for b, back in enumerate((back0, back1)):
+            weave(b, back)
+            for t in (2 * b, 2 * b + 1):
+                nc.scalar.activation(second[:, t, :], h[t][:].indirect(lists[1][:, LAST * P // PER_COLUMN :]), COPY)
         terms = terms_for("terms2", 1, after="terms01_1")
         for t in range(1):
             sum_by_transposes((2,), t, terms[:, t])
@@ -270,17 +273,20 @@ def tile_picked_wlapl_gelu_lo_kernel(
         store_result(0)
         weave(2, back2)
         store_result(1)
-        terms = placed([P, LISTS, PLANES, P], F32, "terms3", 0)
+        terms = placed([P, PLANES, P], F32, "terms3", 0)
         late = sbuf([P, 2 * N], F32, "late", after="zt_bf2")
         with_first = late[:, 0:N].rearrange("p (t v) -> p t v", t=PLANES)
 
-        for d in range(LISTS):
-            for t in range(PLANES):
-                gather(terms[:, d, t, :], t, d, LAST * P, N)
+        for t in range(PLANES):
+            gather(terms[:, t, :], t, 0, LAST * P, N)
+        second_term = sbuf([P, PLANES, P], F32, "second_term")
+        nc.vector.tensor_tensor(
+            second_term[:], second[:], neg_gate[:, 1:2, block(LAST)].to_broadcast([P, PLANES, P]), MULT
+        )
         quantize_z(2)
         second_layer(2, (5, 0))
         for t in range(PLANES):
-            nc.vector.tensor_tensor(with_first[:, t, :], h[t][:, block(LAST)], terms[:, 0, t, :], ADD)
+            nc.vector.tensor_tensor(with_first[:, t, :], h[t][:, block(LAST)], terms[:, t, :], ADD)
         y_bf01 = late[:, N : 2 * N].bitcast(BF16)
         for b in range(2):
             round_result(y_bf01[:, b * N : (b + 1) * N], nc.scalar, acc[b][0])
@@ -291,7 +297,7 @@ def tile_picked_wlapl_gelu_lo_kernel(
             nc.vector.tensor_tensor(
                 z_bf[LAST][:, half].rearrange("p (c i) t -> p c t i", i=LINE),
                 with_first[:, :, half].rearrange("p t (c i) -> p c t i", i=LINE),
-                terms[:, 1, :, half].rearrange("p t (c i) -> p c t i", i=LINE), ADD,
+                second_term[:, :, half].rearrange("p t (c i) -> p c t i", i=LINE), ADD,
             )
         z_mx[LAST] = sbuf([P, P], U32, "z_codes3"), sbuf([P, P], U8, "z_scale3")
         for half in halves:

from contextlib import ExitStack

import concourse.mybir as mybir

F32 = mybir.dt.float32
BF16 = mybir.dt.bfloat16
I32 = mybir.dt.int32
U32 = mybir.dt.uint32
U16 = mybir.dt.uint16
U8 = mybir.dt.uint8
FP8X4 = mybir.dt.float8_e4m3fn_x4
MULT = mybir.AluOpType.mult
ADD = mybir.AluOpType.add
IS_EQUAL = mybir.AluOpType.is_equal
COPY = mybir.ActivationFunctionType.Copy
GELU = mybir.ActivationFunctionType.Gelu_apprx_tanh

P = 128
PLANES = 4
N = 512
QUADRANT = 32
LISTS = 2
PER_COLUMN = 16
LINE = 4
RUN = 8
BLOCKS = 16
LAST = 3
SUMS = {0: (4, 4), 1: (4, 5), 2: (4, 7)}
FLOPS = 2 * 2 * N * N * N


def tile_picked_wlapl_gelu_lo_kernel(
    tc, x_words, x_scales, w1, w2, gate, pos1, pos2, out_0, out_1, out_2
):
    nc = tc.nc
    with ExitStack() as ctx:
        keep = ctx.enter_context(tc.tile_pool(name="keep", bufs=1))
        shared = ctx.enter_context(tc.tile_pool(name="shared", bufs=1))
        banks = ctx.enter_context(tc.psum_pool(name="banks", bufs=1))

        def sbuf(shape, dtype, name, after=None):
            return keep.tile(shape, dtype, name=name, tag=after or name, align_bytes=64)

        def placed(shape, dtype, name, offset):
            return shared.tile(shape, dtype, name=name, align_bytes=64, offset=offset)

        def psum(shape, name, bank):
            return banks.tile(shape, F32, name=name, tag="bank%d" % bank)

        def copy(engine, out, in_):
            if engine is nc.vector:
                nc.vector.tensor_copy(out=out, in_=in_)
            else:
                nc.scalar.copy(out=out, in_=in_)

        def block(b):
            return slice(b * P, (b + 1) * P)

        gate_rows = sbuf([P, 8], F32, "gate_rows")
        gate_run = gate.rearrange("d r v -> (d r) v")[P - 1 : P + 1, :]
        nc.sync.dma_start(out=gate_rows[:], in_=gate_run.rearrange("d (n j) -> (d n) j", j=8))
        w1_raw = sbuf([P, PLANES, N], F32, "w1_raw")
        nc.sync.dma_start(out=w1_raw[:], in_=w1.rearrange("(p j) i -> p j i", j=PLANES))
        x_scale = sbuf([P, N], U8, "x_scale")

        def load_scale_rows(queue, q):
            queue.dma_start(
                out=x_scale[:].bitcast(I32)[QUADRANT * q : QUADRANT * q + 4, :],
                in_=x_scales[0, 4 * q : 4 * q + 4, :].bitcast(I32),
            )

        for q in range(4):
            load_scale_rows(nc.scalar if q % 2 else nc.sync, q)
        x_codes = sbuf([P, N], U32, "x_codes")
        lists = [keep.tile([P, N // PER_COLUMN], U16, name="list%d" % d) for d in range(LISTS)]
        w2_raw = placed([P, PLANES, N], F32, "w2_raw", 0)
        nc.sync.dma_start(out=x_codes[:].bitcast(I32), in_=x_words[0].rearrange("p n t -> p (n t)").bitcast(I32))
        nc.sync.dma_start(lists[0][:], pos1)
        nc.sync.dma_start(lists[1][:], pos2)
        w2_rows = w2.rearrange("(q t r) m -> t q r m", t=PLANES, r=RUN)
        for t in range(PLANES):
            nc.sync.dma_start(out=w2_raw[:, t, :], in_=w2_rows[t])

        ident = sbuf([P, P], F32, "ident")
        ones = sbuf([P, P], F32, "ones")
        column = sbuf([P, P], F32, "column")
        in_quadrant = sbuf([P, QUADRANT], F32, "in_quadrant")
        quadrant_start = sbuf([P, 1], F32, "quadrant_start")
        row = sbuf([P, 1], F32, "row")
        nc.vector.memset(ones[:], 1.0)
        warm = sbuf([P, 1], F32, "warm")
        nc.scalar.activation(warm[:], ones[:, 0:1], GELU)
        nc.vector.tensor_tensor_scan(column[:], ones[:], ones[:], 0.0, MULT, ADD)
        for q in range(4):
            nc.vector.memset(quadrant_start[QUADRANT * q : QUADRANT * (q + 1), :], float(QUADRANT * q))
        nc.vector.transpose(in_quadrant[:], column[:, 0:QUADRANT])
        nc.vector.tensor_tensor(row[:], in_quadrant[:, 0:1], quadrant_start[:], ADD)
        nc.vector.tensor_scalar(ident[:], column[:], row[:, 0:1], None, IS_EQUAL)

        neg_gate = sbuf([P, LISTS, N], F32, "neg_gate")
        for half in range(2):
            spread = psum([P, 4, P], "gate_bank%d" % half, 4 + half)
            for j in range(4):
                col = 4 * half + j
                nc.tensor.transpose(spread[:, j, :], gate_rows[:, col : col + 1].to_broadcast([P, P]), ident[:])
            negated = neg_gate[:].rearrange("p d (n a j) -> p a (d n) j", a=2, j=4)[:, half]
            if half == 1:
                nc.scalar.activation(negated, spread[:].rearrange("p j q -> p q j"), COPY, scale=-1.0)
            else:
                nc.vector.tensor_scalar(negated, spread[:].rearrange("p j q -> p q j"), -1.0, None, MULT)

        def quantize(codes, scale, rounded):
            nc.vector.quantize_mx(out=codes.bitcast(FP8X4), scales=scale, in_=rounded)

        def product(out, w_codes, w_scale, codes, scale):
            nc.tensor.matmul_mx(
                out=out, lhsT=w_codes.bitcast(FP8X4), lhsT_scale=w_scale,
                rhs=codes.bitcast(FP8X4), rhs_scale=scale, start=True, stop=True,
            )

        w1_bf, w1_mx, h = {}, {}, {}

        def round_w1(t, engine, rounded, parts=1):
            w1_bf[t] = rounded
            for n in range(parts):
                runs = slice(n * BLOCKS // parts, (n + 1) * BLOCKS // parts)
                copy(
                    engine,
                    out=w1_bf[t][:].rearrange("p (q a i) j -> p q a j i", a=RUN // LINE, i=LINE)[:, runs],
                    in_=w1_raw[:].rearrange("p j (q t a i) -> p t q a j i", t=PLANES, a=RUN // LINE, i=LINE)[:, t, runs],
                )

        def quantize_w1(t, parts=1):
            codes = sbuf([P, P], U32, "w1_codes%d" % t)
            scale = sbuf([P, P], U8, "w1_scale%d" % t)
            for n in range(parts):
                cols = slice(n * P // parts, (n + 1) * P // parts)
                quantize(codes[:, cols], scale[:, cols], w1_bf[t][:, cols].rearrange("p c j -> p (c j)"))
            w1_mx[t] = codes[:], scale[:]

        def first_layer(t, bank_numbers):
            h[t] = sbuf([P, N], F32, "h%d" % t)
            width = N // len(bank_numbers)
            for n, bank in enumerate(bank_numbers):
                nodes = slice(n * width, (n + 1) * width)
                pre = psum([P, width], "pre%d_%d" % (t, n), bank)
                product(pre[:], w1_mx[t][0], w1_mx[t][1], x_codes[:, nodes], x_scale[:, nodes])
                nc.scalar.activation(h[t][:, nodes], pre[:], GELU)

        zt, z_bf = {}, {}

        def gather(term, t, d, v0, v1):
            window = h[t][:].indirect(lists[d][:, v0 // PER_COLUMN : v1 // PER_COLUMN])
            nc.vector.tensor_tensor(term, window, neg_gate[:, d, v0:v1], MULT)

        def add_turned(b, t, src, own, last):
            count, bank = SUMS[b]
            if own and t == 0:
                zt[b] = psum([P, count * P], "zt%d" % b, bank)
            nc.tensor.matmul(
                zt[b][:, block(t)], lhsT=src, rhs=ident[:], is_transpose=True,
                start=own and t == 0, stop=last and t == count - 1,
            )

        def sum_by_transposes(blocks, t, terms):
            for b in blocks:
                add_turned(b, t, h[t][:, block(b)], True, False)
            for d in range(LISTS):
                gather(terms[:, d, :], t, d, blocks[0] * P, (blocks[-1] + 1) * P)
                for n, b in enumerate(blocks):
                    add_turned(b, t, terms[:, d, block(n)], False, d == LISTS - 1)

        def turn_back(b, bank, rounded):
            halves = SUMS[b][0] // 2
            nc.scalar.copy(
                out=rounded.rearrange("v (u p e) -> v u p e", e=2, p=P),
                in_=zt[b][:].rearrange("v (u e p) -> v u p e", e=2, p=P),
            )
            pairs = rounded.bitcast(F32)
            back = psum([P, halves, P], "back%d" % b, bank)
            for u in range(halves):
                nc.tensor.transpose(back[:, u, :], pairs[:, block(u)], ident[:])
            return back

        def as_pairs(tile):
            return tile[:].rearrange("p v t -> p (v t)").bitcast(F32).rearrange("p (v u) -> p v u", u=2)

        def weave(b, back):
            z_bf[b] = sbuf([P, P, PLANES], BF16, "z_bf%d" % b)
            nc.scalar.copy(out=as_pairs(z_bf[b]), in_=back[:].rearrange("p u v -> p v u"))

        w2_bf = sbuf([P, PLANES, P, PLANES], BF16, "w2_bf")
        w2_codes = sbuf([P, N], U32, "w2_codes")
        w2_scale = sbuf([P, N], U8, "w2_scale")
        y = [sbuf([P, PLANES, P], F32, "y%d" % b)[:] for b in range(N // P)]
        y_scale = sbuf([P, N], U8, "y_scale")
        y_rows = out_0.rearrange("(p t) v -> p t v", t=PLANES)
        y_words = out_1[0].rearrange("p n t -> p (n t)").bitcast(I32)
        z_mx, acc = {}, {}

        def quantize_z(b):
            codes = sbuf([P, P], U32, "z_codes%d" % b)
            scale = sbuf([P, P], U8, "z_scale%d" % b)
            quantize(codes[:], scale[:], z_bf[b][:].rearrange("p v t -> p (v t)"))
            z_mx[b] = codes, scale

        def second_layer(b, bank_numbers):
            per_bank = PLANES // len(bank_numbers)
            acc[b] = [psum([P, per_bank, P], "acc%d_%d" % (b, bank), bank) for bank in bank_numbers]
            for t in range(PLANES):
                product(
                    acc[b][t // per_bank][:, t % per_bank, :],
                    w2_codes[:, block(t)], w2_scale[:, block(t)], z_mx[b][0][:], z_mx[b][1][:],
                )

        def store_result(b):
            per_bank = PLANES // len(acc[b])
            for n, sums in enumerate(acc[b]):
                nc.scalar.copy(out=y[b][:, n * per_bank : (n + 1) * per_bank, :], in_=sums[:])
            nc.sync.dma_start(out=y_rows[:, :, block(b)], in_=y[b])

        def round_result(rounded, engine, src):
            copy(
                engine,
                out=rounded.rearrange("p (c i t) -> p c t i", i=LINE, t=PLANES),
                in_=src[:].rearrange("p t (c i) -> p c t i", i=LINE),
            )

        round_w1(0, nc.vector, sbuf([P, P, PLANES], BF16, "w1_bf0")[:], parts=2)
        round_w1(1, nc.scalar, sbuf([P, P, PLANES], BF16, "w1_bf1")[:])
        quantize_w1(0, parts=2)
        first_layer(0, (0, 1, 7, 4))
        quantize_w1(1)
        first_layer(1, (2,))
        w1_bf23 = sbuf([P, 2 * N], BF16, "w1_bf23", after="w1_bf0")
        for t, bank in ((2, 3), (3, 6)):
            rounded = w1_bf23[:, (t - 2) * N : (t - 1) * N]
            round_w1(t, nc.vector, rounded.rearrange("p (c j) -> p c j", j=PLANES))
            quantize_w1(t)
            first_layer(t, (bank,))

        def terms_for(name, count, after=None):
            return sbuf([P, count, LISTS, P], F32, name, after)

        for t in range(PLANES - 1):
            sum_by_transposes((0, 1), t, sbuf([P, LISTS, 2 * P], F32, "terms01_%d" % t))
        for b in range(2):
            sum_by_transposes((b,), PLANES - 1, terms_for("terms%d_3" % b, 1)[:, 0])
        nc.scalar.copy(
            out=w2_bf[:].rearrange("p t c j -> p c t j"),
            in_=w2_raw[:].rearrange("p j (c t) -> p c t j", t=PLANES),
        )
        zt_bf01 = placed([P, 2 * N], BF16, "zt_bf01", 0)
        back0 = turn_back(0, 1, zt_bf01[:, 0:N])
        back1 = turn_back(1, 2, zt_bf01[:, N : 2 * N])
        second = placed([P, PLANES, P], F32, "second", 2048)
        for b, back in enumerate((back0, back1)):
            weave(b, back)
            for t in (2 * b, 2 * b + 1):
                nc.scalar.activation(second[:, t, :], h[t][:].indirect(lists[1][:, LAST * P // PER_COLUMN :]), COPY)
        terms = terms_for("terms2", 1, after="terms01_1")
        for t in range(1):
            sum_by_transposes((2,), t, terms[:, t])
        quantize(w2_codes[:], w2_scale[:], w2_bf[:].rearrange("p t c j -> p (t c j)"))
        terms = placed([P, 3, LISTS, P], F32, "terms2_late", 4096)
        for t in range(3):
            sum_by_transposes((2,), 1 + t, terms[:, t])
        quantize_z(0)
        second_layer(0, (4,))
        quantize_z(1)
        back2 = turn_back(2, 3, sbuf([P, N], BF16, "zt_bf2")[:])
        second_layer(1, (7,))
        store_result(0)
        weave(2, back2)
        store_result(1)
        terms = placed([P, PLANES, P], F32, "terms3", 0)
        late = sbuf([P, 2 * N], F32, "late", after="zt_bf2")
        with_first = late[:, 0:N].rearrange("p (t v) -> p t v", t=PLANES)

        for t in range(PLANES):
            gather(terms[:, t, :], t, 0, LAST * P, N)
        second_term = sbuf([P, PLANES, P], F32, "second_term")
        nc.vector.tensor_tensor(
            second_term[:], second[:], neg_gate[:, 1:2, block(LAST)].to_broadcast([P, PLANES, P]), MULT
        )
        quantize_z(2)
        second_layer(2, (5, 0))
        for t in range(PLANES):
            nc.vector.tensor_tensor(with_first[:, t, :], h[t][:, block(LAST)], terms[:, t, :], ADD)
        y_bf01 = late[:, N : 2 * N].bitcast(BF16)
        for b in range(2):
            round_result(y_bf01[:, b * N : (b + 1) * N], nc.scalar, acc[b][0])
        store_result(2)
        z_bf[LAST] = sbuf([P, P, PLANES], BF16, "z_bf%d" % LAST)
        halves = [slice(n * P // 2, (n + 1) * P // 2) for n in range(2)]
        for half in halves:
            nc.vector.tensor_tensor(
                z_bf[LAST][:, half].rearrange("p (c i) t -> p c t i", i=LINE),
                with_first[:, :, half].rearrange("p t (c i) -> p c t i", i=LINE),
                second_term[:, :, half].rearrange("p t (c i) -> p c t i", i=LINE), ADD,
            )
        z_mx[LAST] = sbuf([P, P], U32, "z_codes3"), sbuf([P, P], U8, "z_scale3")
        for half in halves:
            quantize(z_mx[LAST][0][:, half], z_mx[LAST][1][:, half], z_bf[LAST][:, half].rearrange("p v t -> p (v t)"))
        second_layer(LAST, (1, 2, 3, 6))
        y_codes = sbuf([P, N], U32, "y_codes")
        for b in range(2):
            quantize(y_codes[:, block(b)], y_scale[:, block(b)], y_bf01[:, b * N : (b + 1) * N])
        nc.sync.dma_start(out=y_words[:, 0 : 2 * P], in_=y_codes[:, 0 : 2 * P].bitcast(I32))
        y_bf2 = sbuf([P, N], BF16, "y_bf2")
        round_result(y_bf2[:], nc.vector, y[2])
        quantize(y_codes[:, block(2)], y_scale[:, block(2)], y_bf2[:])
        for t, sums in enumerate(acc[LAST]):
            nc.scalar.copy(out=y[LAST][:, t : t + 1, :], in_=sums[:])
            if t % 2:
                nc.sync.dma_start(out=y_rows[:, t - 1 : t + 1, block(LAST)], in_=y[LAST][:, t - 1 : t + 1, :])
        y_bf3 = [sbuf([P, N // 2], BF16, "y_bf3_%d" % n) for n in range(2)]
        for n, half in enumerate(halves):
            round_result(y_bf3[n][:], nc.vector, y[LAST][:, :, half])
        for n, half in enumerate(halves):
            cols = slice(LAST * P + half.start, LAST * P + half.stop)
            quantize(y_codes[:, cols], y_scale[:, cols], y_bf3[n][:])
        nc.sync.dma_start(out=y_words[:, 2 * P : N], in_=y_codes[:, 2 * P : N].bitcast(I32))
        for q in range(4):
            queue = nc.scalar if q % 2 else nc.sync
            queue.dma_start(
                out=out_2[0, 4 * q : 4 * q + 4, :].bitcast(I32),
                in_=y_scale[:].bitcast(I32)[QUADRANT * q : QUADRANT * q + 4, :],
            )
